import numpy as np
import ml_dtypes


def mxq(x, axis, fmt="e4m3"):
    dtype, down = {"e4m3": (ml_dtypes.float8_e4m3fn, 7), "e5m2": (ml_dtypes.float8_e5m2, 14)}[fmt]
    v = np.moveaxis(np.asarray(x, np.float32).astype(ml_dtypes.bfloat16).astype(np.float64), axis, -1)
    blocks = v.reshape(v.shape[:-1] + (-1, 32))
    amax = np.abs(blocks).max(-1, keepdims=True)
    byte = np.maximum(np.where(amax > 0, np.frexp(amax)[1] - 1 + 127, 0) - down, 1)
    scale = np.exp2(byte - 127.0)
    codes = (blocks / scale).astype(np.float32).astype(dtype).astype(np.float64)
    return np.moveaxis((codes * scale).reshape(v.shape), -1, axis)


WIDE = False


def mx_kscale(k):
    if not WIDE:
        return np.ones(k)
    levels = np.array([10, -10, 5, -5, 0])
    if k % 512:
        return np.exp2(np.random.permutation(np.resize(levels, k // 32))).repeat(32)
    a = np.empty((k // 512, 16))
    for p in range(k // 512):
        a[p, :8] = np.random.permutation(np.resize(levels, 8))
        for g in range(8):
            far = levels[np.abs(levels - a[p, g]) >= 10]
            a[p, g + 8] = far[np.random.randint(len(far))]
    return np.exp2(a.ravel()).repeat(32)


def f64(x):
    return np.asarray(x).astype(np.float64)


def striped(idx):
    return np.tile(idx.reshape(-1, 16).T, (8, 1)).astype(np.uint16)


def unstriped(offs):
    return offs[:16].T.reshape(-1).astype(np.int64)


E2M1 = np.array([0.0, 0.5, 1.0, 1.5, 2.0, 3.0, 4.0, 6.0, -0.0, -0.5, -1.0, -1.5, -2.0, -3.0, -4.0, -6.0])


def pack_fp4(w):
    k, n = w.shape
    w = f64(np.asarray(w, np.float32).astype(ml_dtypes.bfloat16)).reshape(k // 32, 32, n)
    amax = np.abs(w).max(1)
    mant, ex = np.frexp(amax / 6.0)
    byte = np.clip(np.where(amax > 0, np.where(mant > 0.5, ex, ex - 1) + 127, 1), 1, 254)
    scaled = (w * np.exp2(127.0 - byte)[:, None, :]).reshape(k, n).astype(np.float32)
    c = np.ascontiguousarray(scaled.reshape(k // 512, 128, 4, n).transpose(0, 1, 3, 2)).astype(ml_dtypes.float4_e2m1fn).view(np.uint8) & 0xF
    words = (c[..., 0::2] | (c[..., 1::2] << 4)).reshape(k // 512, 128, 2 * n)
    return np.ascontiguousarray(words), np.ascontiguousarray(byte.astype(np.uint8).reshape(k // 512, 16, n))


def unpack_fp4(words, scales):
    g, _, n = scales.shape
    words = np.ascontiguousarray(words).reshape(g, 128, n, 2)
    nib = np.empty((g, 128, n, 4), np.uint8)
    nib[..., 0::2] = words & 0xF
    nib[..., 1::2] = words >> 4
    vals = E2M1[nib] * np.repeat(np.exp2(scales.astype(np.float64) - 127.0), 8, axis=1)[..., None]
    return vals.transpose(0, 1, 3, 2).reshape(g * 512, n)


K, T, S, H, N = 512, 2048, 512, 512, 128


def setup_inputs():
    n = np.random.standard_normal
    s = mx_kscale(K)[:, None]
    u = mx_kscale(H)
    packed_w2 = pack_fp4(n((H, N)) / np.sqrt(H) / u[:, None])
    return {
        "xT": (n((K, T)) * s).astype(np.float32),
        "w1": (n((K, H)) / np.sqrt(K) / s * u).astype(np.float32),
        "w2_words": packed_w2[0],
        "w2_scales": packed_w2[1],
        "pe": (0.5 * n((H, T)) * u[:, None]).astype(np.float32),
        "offs": striped(np.random.permutation(T)[:S]),
    }


def reference(xT, w1, w2_words, w2_scales, pe, offs):
    xq = mxq(f64(xT)[:, unstriped(offs)], 0, "e4m3")
    g = f64(pe)[:, unstriped(offs)]
    h = (mxq(f64(w1), 0, "e4m3").T @ xq) + g
    return unpack_fp4(w2_words, w2_scales).T @ mxq(h, 0, "e4m3")

@@ -1,0 +1,126 @@
+from contextlib import ExitStack
+
+import concourse.mybir as mybir
+
+K, T, S, H, N = 512, 2048, 512, 512, 128
+FLOPS = 2 * K * H * S + 2 * H * N * S
+
+F32 = mybir.dt.float32
+BF16 = mybir.dt.bfloat16
+I32 = mybir.dt.int32
+U32 = mybir.dt.uint32
+U16 = mybir.dt.uint16
+U8 = mybir.dt.uint8
+FP8X4 = mybir.dt.float8_e4m3fn_x4
+FP4X4 = mybir.dt.float4_e2m1fn_x4
+ADD = mybir.AluOpType.add
+
+P = 128
+PACK = 4
+CHUNK = 128
+CHUNKS = S // CHUNK
+
+
+def tile_picked_posadd_none_l_kernel(tc, xT, w1, w2_words, w2_scales, pe, offs, out):
+    nc = tc.nc
+    with ExitStack() as ctx:
+        keep = ctx.enter_context(tc.tile_pool(name="keep", bufs=1))
+        psum = ctx.enter_context(tc.psum_pool(name="psum", bufs=1))
+
+        offsets = keep.tile([P, S // 16], U16, name="offsets")
+        w1_raw = keep.tile([P, PACK, H], F32, name="w1_raw")
+        x_rows = [keep.tile([P, T], F32, name="x_rows%d" % j) for j in range(PACK)]
+        pe_rows = [keep.tile([P, T], F32, name="pe_rows%d" % t) for t in range(PACK)]
+        w2_codes = keep.tile([P, 2 * N], U8, name="w2_codes", align_bytes=64)
+        w2_plane = keep.tile([P, N], U8, name="w2_plane", align_bytes=64)
+
+        nc.vector.memset(w2_plane[:].bitcast(I32), 0)
+        nc.sync.dma_start(out=w1_raw[:], in_=w1.rearrange("(p j) c -> p j c", j=PACK))
+        nc.sync.dma_start(offsets[:], offs)
+        nc.scalar.dma_start(out=w2_codes[:].bitcast(I32), in_=w2_words[0].bitcast(I32))
+        for q in range(4):
+            nc.scalar.dma_start(
+                out=w2_plane[32 * q : 32 * q + 4, :].bitcast(I32),
+                in_=w2_scales[0, 4 * q : 4 * q + 4, :].bitcast(I32),
+            )
+        x_planes = xT.rearrange("(p j) c -> j p c", j=PACK)
+        pe_planes = pe.rearrange("(p t) c -> t p c", t=PACK)
+        for j in range(PACK):
+            nc.sync.dma_start(out=x_rows[j][:], in_=x_planes[j])
+        for t in range(PACK):
+            nc.sync.dma_start(out=pe_rows[t][:], in_=pe_planes[t])
+
+        w1_grouped = keep.tile([P, H * PACK], BF16, name="w1_grouped", align_bytes=64)
+        nc.vector.tensor_copy(
+            out=w1_grouped[:].rearrange("p (t m j) -> p m j t", t=PACK, j=PACK),
+            in_=w1_raw[:].rearrange("p j (m t) -> p m j t", t=PACK),
+        )
+        w1_codes = keep.tile([P, H], U32, name="w1_codes", align_bytes=64)
+        w1_plane = keep.tile([P, H], U8, name="w1_plane", align_bytes=64)
+        nc.vector.quantize_mx(out=w1_codes[:].bitcast(FP8X4), scales=w1_plane[:], in_=w1_grouped[:])
+
+        x_grouped = keep.tile([P, S, PACK], BF16, name="x_grouped", align_bytes=64)
+        for j in range(PACK):
+            nc.vector.tensor_copy(out=x_grouped[:, :, j], in_=x_rows[j][:].indirect(offsets[:]))
+        x_codes = keep.tile([P, S], U32, name="x_codes", align_bytes=64)
+        x_plane = keep.tile([P, S], U8, name="x_plane", align_bytes=64)
+        nc.vector.quantize_mx(
+            out=x_codes[:].bitcast(FP8X4), scales=x_plane[:], in_=x_grouped[:].rearrange("p s j -> p (s j)")
+        )
+
+        projected = []
+        for t in range(PACK):
+            bank = psum.tile([P, S], F32, name="first_bank%d" % t)
+            cols = slice(t * P, (t + 1) * P)
+            nc.tensor.matmul_mx(
+                out=bank[:],
+                lhsT=w1_codes[:, cols].bitcast(FP8X4),
+                lhsT_scale=w1_plane[:, cols],
+                rhs=x_codes[:].bitcast(FP8X4),
+                rhs_scale=x_plane[:],
+                start=True,
+                stop=True,
+            )
+            staged = keep.tile([P, S], F32, name="projected%d" % t)
+            nc.scalar.copy(out=staged[:], in_=bank[:])
+            projected.append(staged)
+
+        h_low = keep.tile([P, 2, S], F32, name="h_low")
+        h_high = [keep.tile([P, 2, CHUNK], F32, name="h_high%d" % c) for c in range(CHUNKS)]
+        h_grouped = [keep.tile([P, CHUNK, PACK], BF16, name="h_grouped%d" % c, align_bytes=64) for c in range(CHUNKS)]
+        for t in range(2):
+            nc.vector.tensor_tensor(h_low[:, t, :], pe_rows[t][:].indirect(offsets[:]), projected[t][:], ADD)
+        for c in range(CHUNKS):
+            nc.scalar.copy(
+                out=h_grouped[c][:, :, 0:2],
+                in_=h_low[:, :, c * CHUNK : (c + 1) * CHUNK].rearrange("p t s -> p s t"),
+            )
+        for t in range(2, PACK):
+            for c in range(CHUNKS):
+                nc.vector.tensor_tensor(
+                    h_high[c][:, t - 2, :],
+                    pe_rows[t][:].indirect(offsets[:, c * CHUNK // 16 : (c + 1) * CHUNK // 16]),
+                    projected[t][:, c * CHUNK : (c + 1) * CHUNK],
+                    ADD,
+                )
+        for c in range(CHUNKS):
+            nc.scalar.copy(out=h_grouped[c][:, :, 2:4], in_=h_high[c][:].rearrange("p t s -> p s t"))
+        for c in range(CHUNKS):
+            h_codes = keep.tile([P, CHUNK], U32, name="h_codes%d" % c, align_bytes=64)
+            h_plane = keep.tile([P, CHUNK], U8, name="h_plane%d" % c, align_bytes=64)
+            nc.vector.quantize_mx(
+                out=h_codes[:].bitcast(FP8X4), scales=h_plane[:], in_=h_grouped[c][:].rearrange("p s t -> p (s t)")
+            )
+            bank = psum.tile([P, CHUNK], F32, name="second_bank%d" % c)
+            nc.tensor.matmul_mx(
+                out=bank[:],
+                lhsT=w2_codes[:].bitcast(FP4X4),
+                lhsT_scale=w2_plane[:],
+                rhs=h_codes[:].bitcast(FP8X4),
+                rhs_scale=h_plane[:],
+                start=True,
+                stop=True,
+            )
+            result = keep.tile([P, CHUNK], F32, name="result%d" % c)
+            nc.vector.tensor_copy(out=result[:], in_=bank[:])
+            nc.sync.dma_start(out=out[:, c * CHUNK : (c + 1) * CHUNK], in_=result[:])

@@ -103,8 +103,9 @@ def tile_picked_posadd_none_l_kernel(tc, xT, w1, w2_words, w2_scales, pe, offs, 
                     projected[t][:, c * CHUNK : (c + 1) * CHUNK],
                     ADD,
                 )
-        for c in range(CHUNKS):
+        for c in range(CHUNKS - 1):
             nc.scalar.copy(out=h_grouped[c][:, :, 2:4], in_=h_high[c][:].rearrange("p t s -> p s t"))
+        nc.vector.tensor_copy(out=h_grouped[-1][:, :, 2:4], in_=h_high[-1][:].rearrange("p t s -> p s t"))
         for c in range(CHUNKS):
             h_codes = keep.tile([P, CHUNK], U32, name="h_codes%d" % c, align_bytes=64)
             h_plane = keep.tile([P, CHUNK], U8, name="h_plane%d" % c, align_bytes=64)
@@ -122,5 +123,5 @@ def tile_picked_posadd_none_l_kernel(tc, xT, w1, w2_words, w2_scales, pe, offs, 
                 stop=True,
             )
             result = keep.tile([P, CHUNK], F32, name="result%d" % c)
-            nc.vector.tensor_copy(out=result[:], in_=bank[:])
+            nc.scalar.copy(out=result[:], in_=bank[:])
             nc.sync.dma_start(out=out[:, c * CHUNK : (c + 1) * CHUNK], in_=result[:])

@@ -29,83 +29,95 @@ def tile_picked_posadd_none_l_kernel(tc, xT, w1, w2_words, w2_scales, pe, offs, 
 
         offsets = keep.tile([P, S // 16], U16, name="offsets")
         w1_raw = keep.tile([P, PACK, H], F32, name="w1_raw")
-        x_rows = [keep.tile([P, T], F32, name="x_rows%d" % j) for j in range(PACK)]
+        x_pairs = [keep.tile([P, 2, T], F32, name="x_pairs%d" % u) for u in range(2)]
         pe_rows = [keep.tile([P, T], F32, name="pe_rows%d" % t) for t in range(PACK)]
         w2_codes = keep.tile([P, 2 * N], U8, name="w2_codes", align_bytes=64)
         w2_plane = keep.tile([P, N], U8, name="w2_plane", align_bytes=64)
 
         nc.vector.memset(w2_plane[:].bitcast(I32), 0)
-        nc.sync.dma_start(out=w1_raw[:], in_=w1.rearrange("(p j) c -> p j c", j=PACK))
+        x_planes = xT.rearrange("(p u e) c -> u p e c", u=2, e=2)
+        pe_planes = pe.rearrange("(p t) c -> t p c", t=PACK)
+        nc.sync.dma_start(out=x_pairs[0][:], in_=x_planes[0])
         nc.sync.dma_start(offsets[:], offs)
-        nc.scalar.dma_start(out=w2_codes[:].bitcast(I32), in_=w2_words[0].bitcast(I32))
+        nc.sync.dma_start(out=x_pairs[1][:], in_=x_planes[1])
+        nc.sync.dma_start(out=w1_raw[:], in_=w1.rearrange("(p j) c -> p j c", j=PACK))
+        for t in range(PACK):
+            nc.sync.dma_start(out=pe_rows[t][:], in_=pe_planes[t])
+        nc.sync.dma_start(out=w2_codes[:].bitcast(I32), in_=w2_words[0].bitcast(I32))
         for q in range(4):
-            nc.scalar.dma_start(
+            nc.sync.dma_start(
                 out=w2_plane[32 * q : 32 * q + 4, :].bitcast(I32),
                 in_=w2_scales[0, 4 * q : 4 * q + 4, :].bitcast(I32),
             )
-        x_planes = xT.rearrange("(p j) c -> j p c", j=PACK)
-        pe_planes = pe.rearrange("(p t) c -> t p c", t=PACK)
-        for j in range(PACK):
-            nc.sync.dma_start(out=x_rows[j][:], in_=x_planes[j])
-        for t in range(PACK):
-            nc.sync.dma_start(out=pe_rows[t][:], in_=pe_planes[t])
-
-        w1_grouped = keep.tile([P, H * PACK], BF16, name="w1_grouped", align_bytes=64)
-        nc.vector.tensor_copy(
-            out=w1_grouped[:].rearrange("p (t m j) -> p m j t", t=PACK, j=PACK),
-            in_=w1_raw[:].rearrange("p j (m t) -> p m j t", t=PACK),
-        )
-        w1_codes = keep.tile([P, H], U32, name="w1_codes", align_bytes=64)
-        w1_plane = keep.tile([P, H], U8, name="w1_plane", align_bytes=64)
-        nc.vector.quantize_mx(out=w1_codes[:].bitcast(FP8X4), scales=w1_plane[:], in_=w1_grouped[:])
 
         x_grouped = keep.tile([P, S, PACK], BF16, name="x_grouped", align_bytes=64)
         for j in range(PACK):
-            nc.vector.tensor_copy(out=x_grouped[:, :, j], in_=x_rows[j][:].indirect(offsets[:]))
+            nc.vector.tensor_copy(out=x_grouped[:, :, j], in_=x_pairs[j // 2][:, j % 2, :].indirect(offsets[:]))
         x_codes = keep.tile([P, S], U32, name="x_codes", align_bytes=64)
         x_plane = keep.tile([P, S], U8, name="x_plane", align_bytes=64)
         nc.vector.quantize_mx(
             out=x_codes[:].bitcast(FP8X4), scales=x_plane[:], in_=x_grouped[:].rearrange("p s j -> p (s j)")
         )
 
-        projected = []
-        for t in range(PACK):
-            bank = psum.tile([P, S], F32, name="first_bank%d" % t)
-            cols = slice(t * P, (t + 1) * P)
-            nc.tensor.matmul_mx(
-                out=bank[:],
-                lhsT=w1_codes[:, cols].bitcast(FP8X4),
-                lhsT_scale=w1_plane[:, cols],
-                rhs=x_codes[:].bitcast(FP8X4),
-                rhs_scale=x_plane[:],
-                start=True,
-                stop=True,
-            )
-            staged = keep.tile([P, S], F32, name="projected%d" % t)
-            nc.scalar.copy(out=staged[:], in_=bank[:])
-            projected.append(staged)
-
+        w1_grouped = [keep.tile([P, 2 * P * PACK], BF16, name="w1_grouped%d" % u, align_bytes=64) for u in range(2)]
+        w1_codes = [keep.tile([P, 2 * P], U32, name="w1_codes%d" % u, align_bytes=64) for u in range(2)]
+        w1_plane = [keep.tile([P, 2 * P], U8, name="w1_plane%d" % u, align_bytes=64) for u in range(2)]
         h_low = keep.tile([P, 2, S], F32, name="h_low")
+        projected = {}
+        banks = {}
+        for u in range(2):
+            slots = slice(2 * u, 2 * u + 2)
+            nc.scalar.copy(
+                out=w1_grouped[u][:].rearrange("p (t m j) -> p m j t", t=2, j=PACK),
+                in_=w1_raw[:].rearrange("p j (m t) -> p m j t", t=PACK)[:, :, :, slots],
+            )
+        for u in range(2):
+            nc.vector.quantize_mx(out=w1_codes[u][:].bitcast(FP8X4), scales=w1_plane[u][:], in_=w1_grouped[u][:])
+            for t in (2 * u, 2 * u + 1):
+                bank = psum.tile([P, S], F32, name="first_bank%d" % t)
+                cols = slice(t % 2 * P, (t % 2 + 1) * P)
+                nc.tensor.matmul_mx(
+                    out=bank[:],
+                    lhsT=w1_codes[u][:, cols].bitcast(FP8X4),
+                    lhsT_scale=w1_plane[u][:, cols],
+                    rhs=x_codes[:].bitcast(FP8X4),
+                    rhs_scale=x_plane[:],
+                    start=True,
+                    stop=True,
+                )
+                banks[t] = bank
+            picked = keep.tile([P, S], F32, name="w1_grouped%d" % u, align_bytes=64)
+            nc.vector.tensor_copy(out=picked[:], in_=pe_rows[u][:].indirect(offsets[:]))
+            nc.vector.tensor_tensor(h_low[:, u, :], banks[u][:], picked[:], ADD)
+        for t in (2, 3):
+            staged = keep.tile([P, S], F32, name="projected%d" % t)
+            nc.scalar.copy(out=staged[:], in_=banks[t][:])
+            projected[t] = staged
+
         h_high = [keep.tile([P, 2, CHUNK], F32, name="h_high%d" % c) for c in range(CHUNKS)]
         h_grouped = [keep.tile([P, CHUNK, PACK], BF16, name="h_grouped%d" % c, align_bytes=64) for c in range(CHUNKS)]
-        for t in range(2):
-            nc.vector.tensor_tensor(h_low[:, t, :], pe_rows[t][:].indirect(offsets[:]), projected[t][:], ADD)
         for c in range(CHUNKS):
             nc.scalar.copy(
                 out=h_grouped[c][:, :, 0:2],
                 in_=h_low[:, :, c * CHUNK : (c + 1) * CHUNK].rearrange("p t s -> p s t"),
             )
+        half = CHUNK // 2
+        pieces = [(c, 0, CHUNK) for c in range(CHUNKS - 1)] + [(CHUNKS - 1, 0, half), (CHUNKS - 1, half, CHUNK)]
         for t in range(2, PACK):
-            for c in range(CHUNKS):
+            for c, lo, hi in pieces if t == PACK - 1 else [(c, 0, CHUNK) for c in range(CHUNKS)]:
                 nc.vector.tensor_tensor(
-                    h_high[c][:, t - 2, :],
-                    pe_rows[t][:].indirect(offsets[:, c * CHUNK // 16 : (c + 1) * CHUNK // 16]),
-                    projected[t][:, c * CHUNK : (c + 1) * CHUNK],
+                    h_high[c][:, t - 2, lo:hi],
+                    pe_rows[t][:].indirect(offsets[:, (c * CHUNK + lo) // 16 : (c * CHUNK + hi) // 16]),
+                    projected[t][:, c * CHUNK + lo : c * CHUNK + hi],
                     ADD,
                 )
-        for c in range(CHUNKS - 1):
-            nc.scalar.copy(out=h_grouped[c][:, :, 2:4], in_=h_high[c][:].rearrange("p t s -> p s t"))
-        nc.vector.tensor_copy(out=h_grouped[-1][:, :, 2:4], in_=h_high[-1][:].rearrange("p t s -> p s t"))
+        for n, (c, lo, hi) in enumerate(pieces):
+            dst = h_grouped[c][:, lo:hi, 2:4]
+            src = h_high[c][:, :, lo:hi].rearrange("p t s -> p s t")
+            if n == len(pieces) - 2:
+                nc.vector.tensor_copy(out=dst, in_=src)
+            else:
+                nc.scalar.copy(out=dst, in_=src)
         for c in range(CHUNKS):
             h_codes = keep.tile([P, CHUNK], U32, name="h_codes%d" % c, align_bytes=64)
             h_plane = keep.tile([P, CHUNK], U8, name="h_plane%d" % c, align_bytes=64)
@@ -123,5 +135,8 @@ def tile_picked_posadd_none_l_kernel(tc, xT, w1, w2_words, w2_scales, pe, offs, 
                 stop=True,
             )
             result = keep.tile([P, CHUNK], F32, name="result%d" % c)
-            nc.scalar.copy(out=result[:], in_=bank[:])
+            if c == CHUNKS - 1:
+                nc.vector.tensor_copy(out=result[:], in_=bank[:])
+            else:
+                nc.scalar.copy(out=result[:], in_=bank[:])
             nc.sync.dma_start(out=out[:, c * CHUNK : (c + 1) * CHUNK], in_=result[:])

@@ -94,7 +94,7 @@ def tile_picked_posadd_none_l_kernel(tc, xT, w1, w2_words, w2_scales, pe, offs, 
             nc.scalar.copy(out=staged[:], in_=banks[t][:])
             projected[t] = staged
 
-        h_high = [keep.tile([P, 2, CHUNK], F32, name="h_high%d" % c) for c in range(CHUNKS)]
+        h_high = keep.tile([P, 2, S], F32, name="h_high")
         h_grouped = [keep.tile([P, CHUNK, PACK], BF16, name="h_grouped%d" % c, align_bytes=64) for c in range(CHUNKS)]
         for c in range(CHUNKS):
             nc.scalar.copy(
@@ -103,21 +103,22 @@ def tile_picked_posadd_none_l_kernel(tc, xT, w1, w2_words, w2_scales, pe, offs, 
             )
         half = CHUNK // 2
         pieces = [(c, 0, CHUNK) for c in range(CHUNKS - 1)] + [(CHUNKS - 1, 0, half), (CHUNKS - 1, half, CHUNK)]
-        for t in range(2, PACK):
-            for c, lo, hi in pieces if t == PACK - 1 else [(c, 0, CHUNK) for c in range(CHUNKS)]:
-                nc.vector.tensor_tensor(
-                    h_high[c][:, t - 2, lo:hi],
-                    pe_rows[t][:].indirect(offsets[:, (c * CHUNK + lo) // 16 : (c * CHUNK + hi) // 16]),
-                    projected[t][:, c * CHUNK + lo : c * CHUNK + hi],
-                    ADD,
-                )
+        nc.vector.tensor_tensor(h_high[:, 0, :], pe_rows[2][:].indirect(offsets[:]), projected[2][:], ADD)
+        for c, lo, hi in pieces:
+            nc.vector.tensor_tensor(
+                h_high[:, 1, c * CHUNK + lo : c * CHUNK + hi],
+                pe_rows[3][:].indirect(offsets[:, (c * CHUNK + lo) // 16 : (c * CHUNK + hi) // 16]),
+                projected[3][:, c * CHUNK + lo : c * CHUNK + hi],
+                ADD,
+            )
         for n, (c, lo, hi) in enumerate(pieces):
             dst = h_grouped[c][:, lo:hi, 2:4]
-            src = h_high[c][:, :, lo:hi].rearrange("p t s -> p s t")
+            src = h_high[:, :, c * CHUNK + lo : c * CHUNK + hi].rearrange("p t s -> p s t")
             if n == len(pieces) - 2:
                 nc.vector.tensor_copy(out=dst, in_=src)
             else:
                 nc.scalar.copy(out=dst, in_=src)
+        result = keep.tile([P, S], F32, name="result")
         for c in range(CHUNKS):
             h_codes = keep.tile([P, CHUNK], U32, name="h_codes%d" % c, align_bytes=64)
             h_plane = keep.tile([P, CHUNK], U8, name="h_plane%d" % c, align_bytes=64)
@@ -134,9 +135,11 @@ def tile_picked_posadd_none_l_kernel(tc, xT, w1, w2_words, w2_scales, pe, offs, 
                 start=True,
                 stop=True,
             )
-            result = keep.tile([P, CHUNK], F32, name="result%d" % c)
+            cols = slice(c * CHUNK, (c + 1) * CHUNK)
             if c == CHUNKS - 1:
-                nc.vector.tensor_copy(out=result[:], in_=bank[:])
+                nc.vector.tensor_copy(out=result[:, cols], in_=bank[:])
             else:
-                nc.scalar.copy(out=result[:], in_=bank[:])
-            nc.sync.dma_start(out=out[:, c * CHUNK : (c + 1) * CHUNK], in_=result[:])
+                nc.scalar.copy(out=result[:, cols], in_=bank[:])
+            if c != CHUNKS - 2:
+                stored = slice((c - 1) * CHUNK, S) if c == CHUNKS - 1 else cols
+                nc.sync.dma_start(out=out[:, stored], in_=result[:, stored])

@@ -140,6 +140,6 @@ def tile_picked_posadd_none_l_kernel(tc, xT, w1, w2_words, w2_scales, pe, offs, 
                 nc.vector.tensor_copy(out=result[:, cols], in_=bank[:])
             else:
                 nc.scalar.copy(out=result[:, cols], in_=bank[:])
-            if c != CHUNKS - 2:
-                stored = slice((c - 1) * CHUNK, S) if c == CHUNKS - 1 else cols
+            if c > 0:
+                stored = slice(0, 2 * CHUNK) if c == 1 else cols
                 nc.sync.dma_start(out=out[:, stored], in_=result[:, stored])

@@ -104,20 +104,25 @@ def tile_picked_posadd_none_l_kernel(tc, xT, w1, w2_words, w2_scales, pe, offs, 
         half = CHUNK // 2
         pieces = [(c, 0, CHUNK) for c in range(CHUNKS - 1)] + [(CHUNKS - 1, 0, half), (CHUNKS - 1, half, CHUNK)]
         nc.vector.tensor_tensor(h_high[:, 0, :], pe_rows[2][:].indirect(offsets[:]), projected[2][:], ADD)
-        for c, lo, hi in pieces:
+        for c, lo, hi in pieces[:-1]:
             nc.vector.tensor_tensor(
                 h_high[:, 1, c * CHUNK + lo : c * CHUNK + hi],
                 pe_rows[3][:].indirect(offsets[:, (c * CHUNK + lo) // 16 : (c * CHUNK + hi) // 16]),
                 projected[3][:, c * CHUNK + lo : c * CHUNK + hi],
                 ADD,
             )
-        for n, (c, lo, hi) in enumerate(pieces):
-            dst = h_grouped[c][:, lo:hi, 2:4]
-            src = h_high[:, :, c * CHUNK + lo : c * CHUNK + hi].rearrange("p t s -> p s t")
-            if n == len(pieces) - 2:
-                nc.vector.tensor_copy(out=dst, in_=src)
-            else:
-                nc.scalar.copy(out=dst, in_=src)
+        for c, lo, hi in pieces[:-1]:
+            nc.scalar.copy(
+                out=h_grouped[c][:, lo:hi, 2:4],
+                in_=h_high[:, :, c * CHUNK + lo : c * CHUNK + hi].rearrange("p t s -> p s t"),
+            )
+        nc.vector.tensor_tensor(
+            h_high[:, 1, 0:half], pe_rows[3][:].indirect(offsets[:, (S - half) // 16 :]), projected[3][:, S - half :], ADD
+        )
+        flat = h_high[:].rearrange("p t s -> p (t s)")
+        nc.vector.tensor_copy(
+            out=h_grouped[-1][:, half:, 2:4], in_=flat[:, S - half : S + half].rearrange("p (t s) -> p s t", t=2)
+        )
         result = keep.tile([P, S], F32, name="result")
         for c in range(CHUNKS):
             h_codes = keep.tile([P, CHUNK], U32, name="h_codes%d" % c, align_bytes=64)
@@ -136,7 +141,7 @@ def tile_picked_posadd_none_l_kernel(tc, xT, w1, w2_words, w2_scales, pe, offs, 
                 stop=True,
             )
             cols = slice(c * CHUNK, (c + 1) * CHUNK)
-            if c == CHUNKS - 1:
+            if c >= CHUNKS - 2:
                 nc.vector.tensor_copy(out=result[:, cols], in_=bank[:])
             else:
                 nc.scalar.copy(out=result[:, cols], in_=bank[:])

@@ -35,6 +35,11 @@ def tile_picked_posadd_none_l_kernel(tc, xT, w1, w2_words, w2_scales, pe, offs, 
         w2_plane = keep.tile([P, N], U8, name="w2_plane", align_bytes=64)
 
         nc.vector.memset(w2_plane[:].bitcast(I32), 0)
+        for q in range(4):
+            nc.scalar.dma_start(
+                out=w2_plane[32 * q : 32 * q + 4, :].bitcast(I32),
+                in_=w2_scales[0, 4 * q : 4 * q + 4, :].bitcast(I32),
+            )
         x_planes = xT.rearrange("(p u e) c -> u p e c", u=2, e=2)
         pe_planes = pe.rearrange("(p t) c -> t p c", t=PACK)
         nc.sync.dma_start(out=x_pairs[0][:], in_=x_planes[0])
@@ -44,11 +49,6 @@ def tile_picked_posadd_none_l_kernel(tc, xT, w1, w2_words, w2_scales, pe, offs, 
         for t in range(PACK):
             nc.sync.dma_start(out=pe_rows[t][:], in_=pe_planes[t])
         nc.sync.dma_start(out=w2_codes[:].bitcast(I32), in_=w2_words[0].bitcast(I32))
-        for q in range(4):
-            nc.sync.dma_start(
-                out=w2_plane[32 * q : 32 * q + 4, :].bitcast(I32),
-                in_=w2_scales[0, 4 * q : 4 * q + 4, :].bitcast(I32),
-            )
 
         x_grouped = keep.tile([P, S, PACK], BF16, name="x_grouped", align_bytes=64)
         for j in range(PACK):

@@ -16,9 +16,13 @@ FP4X4 = mybir.dt.float4_e2m1fn_x4
 ADD = mybir.AluOpType.add
 
 P = 128
-PACK = 4
+SLOTS = 4
+PAIRS = 2
+PER_COLUMN = 16
+QUADRANTS = 4
 CHUNK = 128
 CHUNKS = S // CHUNK
+OWN = CHUNK // 2
 
 
 def tile_picked_posadd_none_l_kernel(tc, xT, w1, w2_words, w2_scales, pe, offs, out):
@@ -27,124 +31,130 @@ def tile_picked_posadd_none_l_kernel(tc, xT, w1, w2_words, w2_scales, pe, offs, 
         keep = ctx.enter_context(tc.tile_pool(name="keep", bufs=1))
         psum = ctx.enter_context(tc.psum_pool(name="psum", bufs=1))
 
-        offsets = keep.tile([P, S // 16], U16, name="offsets")
-        w1_raw = keep.tile([P, PACK, H], F32, name="w1_raw")
-        x_pairs = [keep.tile([P, 2, T], F32, name="x_pairs%d" % u) for u in range(2)]
-        pe_rows = [keep.tile([P, T], F32, name="pe_rows%d" % t) for t in range(PACK)]
+        offsets = keep.tile([P, S // PER_COLUMN], U16, name="offsets")
+        w1_raw = keep.tile([P, SLOTS, H], F32, name="w1_raw")
+        x_pairs = [keep.tile([P, 2, T], F32, name="x_pairs%d" % u) for u in range(PAIRS)]
+        pe_rows = [keep.tile([P, T], F32, name="pe_rows%d" % s) for s in range(SLOTS)]
         w2_codes = keep.tile([P, 2 * N], U8, name="w2_codes", align_bytes=64)
-        w2_plane = keep.tile([P, N], U8, name="w2_plane", align_bytes=64)
+        w2_scale_tile = keep.tile([P, N], U8, name="w2_scale_tile", align_bytes=64)
 
-        nc.vector.memset(w2_plane[:].bitcast(I32), 0)
-        for q in range(4):
+        def entries(tokens):
+            return offsets[:, tokens.start // PER_COLUMN : tokens.stop // PER_COLUMN]
+
+        nc.vector.memset(w2_scale_tile[:].bitcast(I32), 0)
+        for q in range(QUADRANTS):
             nc.scalar.dma_start(
-                out=w2_plane[32 * q : 32 * q + 4, :].bitcast(I32),
+                out=w2_scale_tile[32 * q : 32 * q + 4, :].bitcast(I32),
                 in_=w2_scales[0, 4 * q : 4 * q + 4, :].bitcast(I32),
             )
-        x_planes = xT.rearrange("(p u e) c -> u p e c", u=2, e=2)
-        pe_planes = pe.rearrange("(p t) c -> t p c", t=PACK)
-        nc.sync.dma_start(out=x_pairs[0][:], in_=x_planes[0])
+
+        x_by_pair = xT.rearrange("(p u e) c -> u p e c", u=PAIRS, e=2)
+        pe_by_slot = pe.rearrange("(p s) c -> s p c", s=SLOTS)
+        nc.sync.dma_start(out=x_pairs[0][:], in_=x_by_pair[0])
         nc.sync.dma_start(offsets[:], offs)
-        nc.sync.dma_start(out=x_pairs[1][:], in_=x_planes[1])
-        nc.sync.dma_start(out=w1_raw[:], in_=w1.rearrange("(p j) c -> p j c", j=PACK))
-        for t in range(PACK):
-            nc.sync.dma_start(out=pe_rows[t][:], in_=pe_planes[t])
+        nc.sync.dma_start(out=x_pairs[1][:], in_=x_by_pair[1])
+        nc.sync.dma_start(out=w1_raw[:], in_=w1.rearrange("(p j) c -> p j c", j=SLOTS))
+        for s in range(SLOTS):
+            nc.sync.dma_start(out=pe_rows[s][:], in_=pe_by_slot[s])
         nc.sync.dma_start(out=w2_codes[:].bitcast(I32), in_=w2_words[0].bitcast(I32))
 
-        x_grouped = keep.tile([P, S, PACK], BF16, name="x_grouped", align_bytes=64)
-        for j in range(PACK):
-            nc.vector.tensor_copy(out=x_grouped[:, :, j], in_=x_pairs[j // 2][:, j % 2, :].indirect(offsets[:]))
+        x_grouped = keep.tile([P, S, SLOTS], BF16, name="x_grouped", align_bytes=64)
+        for s in range(SLOTS):
+            nc.vector.tensor_copy(out=x_grouped[:, :, s], in_=x_pairs[s // 2][:, s % 2, :].indirect(offsets[:]))
         x_codes = keep.tile([P, S], U32, name="x_codes", align_bytes=64)
-        x_plane = keep.tile([P, S], U8, name="x_plane", align_bytes=64)
+        x_scale_tile = keep.tile([P, S], U8, name="x_scale_tile", align_bytes=64)
         nc.vector.quantize_mx(
-            out=x_codes[:].bitcast(FP8X4), scales=x_plane[:], in_=x_grouped[:].rearrange("p s j -> p (s j)")
+            out=x_codes[:].bitcast(FP8X4), scales=x_scale_tile[:], in_=x_grouped[:].rearrange("p c s -> p (c s)")
         )
 
-        w1_grouped = [keep.tile([P, 2 * P * PACK], BF16, name="w1_grouped%d" % u, align_bytes=64) for u in range(2)]
-        w1_codes = [keep.tile([P, 2 * P], U32, name="w1_codes%d" % u, align_bytes=64) for u in range(2)]
-        w1_plane = [keep.tile([P, 2 * P], U8, name="w1_plane%d" % u, align_bytes=64) for u in range(2)]
+        w1_grouped = [
+            keep.tile([P, 2 * P * SLOTS], BF16, name="w1_grouped%d" % u, tag="pair%d" % u, align_bytes=64)
+            for u in range(PAIRS)
+        ]
+        w1_codes = [keep.tile([P, 2 * P], U32, name="w1_codes%d" % u, align_bytes=64) for u in range(PAIRS)]
+        w1_scale_tile = [keep.tile([P, 2 * P], U8, name="w1_scale_tile%d" % u, align_bytes=64) for u in range(PAIRS)]
         h_low = keep.tile([P, 2, S], F32, name="h_low")
-        projected = {}
-        banks = {}
-        for u in range(2):
-            slots = slice(2 * u, 2 * u + 2)
+        for u in range(PAIRS):
             nc.scalar.copy(
-                out=w1_grouped[u][:].rearrange("p (t m j) -> p m j t", t=2, j=PACK),
-                in_=w1_raw[:].rearrange("p j (m t) -> p m j t", t=PACK)[:, :, :, slots],
+                out=w1_grouped[u][:].rearrange("p (e m j) -> p m j e", e=2, j=SLOTS),
+                in_=w1_raw[:].rearrange("p j (m s) -> p m j s", s=SLOTS)[:, :, :, 2 * u : 2 * u + 2],
             )
-        for u in range(2):
-            nc.vector.quantize_mx(out=w1_codes[u][:].bitcast(FP8X4), scales=w1_plane[u][:], in_=w1_grouped[u][:])
-            for t in (2 * u, 2 * u + 1):
-                bank = psum.tile([P, S], F32, name="first_bank%d" % t)
-                cols = slice(t % 2 * P, (t % 2 + 1) * P)
+
+        first_banks = []
+        for u in range(PAIRS):
+            nc.vector.quantize_mx(out=w1_codes[u][:].bitcast(FP8X4), scales=w1_scale_tile[u][:], in_=w1_grouped[u][:])
+            for e in range(2):
+                first_bank = psum.tile([P, S], F32, name="first_bank%d" % (2 * u + e))
                 nc.tensor.matmul_mx(
-                    out=bank[:],
-                    lhsT=w1_codes[u][:, cols].bitcast(FP8X4),
-                    lhsT_scale=w1_plane[u][:, cols],
+                    out=first_bank[:],
+                    lhsT=w1_codes[u][:, e * P : (e + 1) * P].bitcast(FP8X4),
+                    lhsT_scale=w1_scale_tile[u][:, e * P : (e + 1) * P],
                     rhs=x_codes[:].bitcast(FP8X4),
-                    rhs_scale=x_plane[:],
+                    rhs_scale=x_scale_tile[:],
                     start=True,
                     stop=True,
                 )
-                banks[t] = bank
-            picked = keep.tile([P, S], F32, name="w1_grouped%d" % u, align_bytes=64)
+                first_banks.append(first_bank)
+            picked = keep.tile([P, S], F32, name="picked%d" % u, tag="pair%d" % u, align_bytes=64)
             nc.vector.tensor_copy(out=picked[:], in_=pe_rows[u][:].indirect(offsets[:]))
-            nc.vector.tensor_tensor(h_low[:, u, :], banks[u][:], picked[:], ADD)
-        for t in (2, 3):
-            staged = keep.tile([P, S], F32, name="projected%d" % t)
-            nc.scalar.copy(out=staged[:], in_=banks[t][:])
-            projected[t] = staged
+            nc.vector.tensor_tensor(h_low[:, u, :], first_banks[u][:], picked[:], ADD)
+
+        projected = {}
+        for s in (2, 3):
+            projected[s] = keep.tile([P, S], F32, name="projected%d" % s)
+            nc.scalar.copy(out=projected[s][:], in_=first_banks[s][:])
 
         h_high = keep.tile([P, 2, S], F32, name="h_high")
-        h_grouped = [keep.tile([P, CHUNK, PACK], BF16, name="h_grouped%d" % c, align_bytes=64) for c in range(CHUNKS)]
-        for c in range(CHUNKS):
-            nc.scalar.copy(
-                out=h_grouped[c][:, :, 0:2],
-                in_=h_low[:, :, c * CHUNK : (c + 1) * CHUNK].rearrange("p t s -> p s t"),
-            )
-        half = CHUNK // 2
-        pieces = [(c, 0, CHUNK) for c in range(CHUNKS - 1)] + [(CHUNKS - 1, 0, half), (CHUNKS - 1, half, CHUNK)]
+        h_grouped = [keep.tile([P, CHUNK, SLOTS], BF16, name="h_grouped%d" % c, align_bytes=64) for c in range(CHUNKS)]
+        chunks = [slice(c * CHUNK, (c + 1) * CHUNK) for c in range(CHUNKS)]
+        for c, tokens in enumerate(chunks):
+            nc.scalar.copy(out=h_grouped[c][:, :, 0:2], in_=h_low[:, :, tokens].rearrange("p e c -> p c e"))
         nc.vector.tensor_tensor(h_high[:, 0, :], pe_rows[2][:].indirect(offsets[:]), projected[2][:], ADD)
-        for c, lo, hi in pieces[:-1]:
+
+        by_scalar = chunks[:-1] + [slice(chunks[-1].start, S - OWN)]
+        for tokens in by_scalar:
             nc.vector.tensor_tensor(
-                h_high[:, 1, c * CHUNK + lo : c * CHUNK + hi],
-                pe_rows[3][:].indirect(offsets[:, (c * CHUNK + lo) // 16 : (c * CHUNK + hi) // 16]),
-                projected[3][:, c * CHUNK + lo : c * CHUNK + hi],
-                ADD,
+                h_high[:, 1, tokens], pe_rows[3][:].indirect(entries(tokens)), projected[3][:, tokens], ADD
             )
-        for c, lo, hi in pieces[:-1]:
+        for c, tokens in enumerate(by_scalar):
             nc.scalar.copy(
-                out=h_grouped[c][:, lo:hi, 2:4],
-                in_=h_high[:, :, c * CHUNK + lo : c * CHUNK + hi].rearrange("p t s -> p s t"),
+                out=h_grouped[c][:, 0 : tokens.stop - tokens.start, 2:4],
+                in_=h_high[:, :, tokens].rearrange("p e c -> p c e"),
             )
-        nc.vector.tensor_tensor(
-            h_high[:, 1, 0:half], pe_rows[3][:].indirect(offsets[:, (S - half) // 16 :]), projected[3][:, S - half :], ADD
-        )
-        flat = h_high[:].rearrange("p t s -> p (t s)")
+
+        own = slice(S - OWN, S)
+        nc.vector.tensor_tensor(h_high[:, 1, 0:OWN], pe_rows[3][:].indirect(entries(own)), projected[3][:, own], ADD)
+        h_high_row = h_high[:].rearrange("p e c -> p (e c)")
         nc.vector.tensor_copy(
-            out=h_grouped[-1][:, half:, 2:4], in_=flat[:, S - half : S + half].rearrange("p (t s) -> p s t", t=2)
+            out=h_grouped[-1][:, CHUNK - OWN :, 2:4],
+            in_=h_high_row[:, S - OWN : S + OWN].rearrange("p (e c) -> p c e", e=2),
         )
+
         result = keep.tile([P, S], F32, name="result")
-        for c in range(CHUNKS):
+        for c, tokens in enumerate(chunks):
             h_codes = keep.tile([P, CHUNK], U32, name="h_codes%d" % c, align_bytes=64)
-            h_plane = keep.tile([P, CHUNK], U8, name="h_plane%d" % c, align_bytes=64)
-            nc.vector.quantize_mx(
-                out=h_codes[:].bitcast(FP8X4), scales=h_plane[:], in_=h_grouped[c][:].rearrange("p s t -> p (s t)")
-            )
-            bank = psum.tile([P, CHUNK], F32, name="second_bank%d" % c)
+            h_scale_tile = keep.tile([P, CHUNK], U8, name="h_scale_tile%d" % c, align_bytes=64)
+            last = c == CHUNKS - 1
+            for part in [slice(0, CHUNK - OWN), slice(CHUNK - OWN, CHUNK)] if last else [slice(0, CHUNK)]:
+                nc.vector.quantize_mx(
+                    out=h_codes[:, part].bitcast(FP8X4),
+                    scales=h_scale_tile[:, part],
+                    in_=h_grouped[c][:, part, :].rearrange("p c s -> p (c s)"),
+                )
+            second_bank = psum.tile([P, CHUNK], F32, name="second_bank%d" % c)
             nc.tensor.matmul_mx(
-                out=bank[:],
+                out=second_bank[:],
                 lhsT=w2_codes[:].bitcast(FP4X4),
-                lhsT_scale=w2_plane[:],
+                lhsT_scale=w2_scale_tile[:],
                 rhs=h_codes[:].bitcast(FP8X4),
-                rhs_scale=h_plane[:],
+                rhs_scale=h_scale_tile[:],
                 start=True,
                 stop=True,
             )
-            cols = slice(c * CHUNK, (c + 1) * CHUNK)
-            if c >= CHUNKS - 2:
-                nc.vector.tensor_copy(out=result[:, cols], in_=bank[:])
+            if c >= CHUNKS // 2:
+                nc.vector.tensor_copy(out=result[:, tokens], in_=second_bank[:])
             else:
-                nc.scalar.copy(out=result[:, cols], in_=bank[:])
+                nc.scalar.copy(out=result[:, tokens], in_=second_bank[:])
             if c > 0:
-                stored = slice(0, 2 * CHUNK) if c == 1 else cols
+                stored = slice(0, tokens.stop) if c == 1 else tokens
                 nc.sync.dma_start(out=out[:, stored], in_=result[:, stored])

@@ -34,7 +34,8 @@ def tile_picked_posadd_none_l_kernel(tc, xT, w1, w2_words, w2_scales, pe, offs, 
         offsets = keep.tile([P, S // PER_COLUMN], U16, name="offsets")
         w1_raw = keep.tile([P, SLOTS, H], F32, name="w1_raw")
         x_pairs = [keep.tile([P, 2, T], F32, name="x_pairs%d" % u) for u in range(PAIRS)]
-        pe_rows = [keep.tile([P, T], F32, name="pe_rows%d" % s) for s in range(SLOTS)]
+        pe_low = keep.tile([P, 2, T], F32, name="pe_low")
+        pe_rows = {s: keep.tile([P, T], F32, name="pe_rows%d" % s) for s in (2, 3)}
         w2_codes = keep.tile([P, 2 * N], U8, name="w2_codes", align_bytes=64)
         w2_scale_tile = keep.tile([P, N], U8, name="w2_scale_tile", align_bytes=64)
 
@@ -54,7 +55,8 @@ def tile_picked_posadd_none_l_kernel(tc, xT, w1, w2_words, w2_scales, pe, offs, 
         nc.sync.dma_start(offsets[:], offs)
         nc.sync.dma_start(out=x_pairs[1][:], in_=x_by_pair[1])
         nc.sync.dma_start(out=w1_raw[:], in_=w1.rearrange("(p j) c -> p j c", j=SLOTS))
-        for s in range(SLOTS):
+        nc.sync.dma_start(out=pe_low[:], in_=pe.rearrange("(p u e) c -> u p e c", u=PAIRS, e=2)[0])
+        for s in (2, 3):
             nc.sync.dma_start(out=pe_rows[s][:], in_=pe_by_slot[s])
         nc.sync.dma_start(out=w2_codes[:].bitcast(I32), in_=w2_words[0].bitcast(I32))
 
@@ -68,7 +70,7 @@ def tile_picked_posadd_none_l_kernel(tc, xT, w1, w2_words, w2_scales, pe, offs, 
         )
 
         w1_grouped = [
-            keep.tile([P, 2 * P * SLOTS], BF16, name="w1_grouped%d" % u, tag="pair%d" % u, align_bytes=64)
+            keep.tile([P, 2 * P * SLOTS], BF16, name="w1_grouped%d" % u, align_bytes=64)
             for u in range(PAIRS)
         ]
         w1_codes = [keep.tile([P, 2 * P], U32, name="w1_codes%d" % u, align_bytes=64) for u in range(PAIRS)]
@@ -95,21 +97,31 @@ def tile_picked_posadd_none_l_kernel(tc, xT, w1, w2_words, w2_scales, pe, offs, 
                     stop=True,
                 )
                 first_banks.append(first_bank)
-            picked = keep.tile([P, S], F32, name="picked%d" % u, tag="pair%d" % u, align_bytes=64)
-            nc.vector.tensor_copy(out=picked[:], in_=pe_rows[u][:].indirect(offsets[:]))
-            nc.vector.tensor_tensor(h_low[:, u, :], first_banks[u][:], picked[:], ADD)
 
-        projected = {}
-        for s in (2, 3):
-            projected[s] = keep.tile([P, S], F32, name="projected%d" % s)
-            nc.scalar.copy(out=projected[s][:], in_=first_banks[s][:])
+        projected_low = keep.tile([P, 2, S], F32, name="projected_low")
+        for s in (0, 1):
+            nc.scalar.copy(out=projected_low[:, s, :], in_=first_banks[s][:])
+        projected = {3: keep.tile([P, S], F32, name="projected3")}
+        nc.scalar.copy(out=projected[3][:], in_=first_banks[3][:])
 
         h_high = keep.tile([P, 2, S], F32, name="h_high")
         h_grouped = [keep.tile([P, CHUNK, SLOTS], BF16, name="h_grouped%d" % c, align_bytes=64) for c in range(CHUNKS)]
         chunks = [slice(c * CHUNK, (c + 1) * CHUNK) for c in range(CHUNKS)]
+        for half in range(2):
+            tokens = slice(half * S // 2, (half + 1) * S // 2)
+            picked_low = keep.tile([P, 2, S // 2], F32, name="picked_low%d" % half)
+            for s in (0, 1):
+                nc.vector.tensor_copy(out=picked_low[:, s, :], in_=pe_low[:, s, :].indirect(entries(tokens)))
+                nc.gpsimd.tensor_tensor(h_low[:, s, tokens], picked_low[:, s, :], projected_low[:, s, tokens], ADD)
         for c, tokens in enumerate(chunks):
             nc.scalar.copy(out=h_grouped[c][:, :, 0:2], in_=h_low[:, :, tokens].rearrange("p e c -> p c e"))
-        nc.vector.tensor_tensor(h_high[:, 0, :], pe_rows[2][:].indirect(offsets[:]), projected[2][:], ADD)
+
+        picked2 = keep.tile([P, S], F32, name="picked2")
+        token_halves = [slice(0, S // 2), slice(S // 2, S)]
+        for tokens in token_halves:
+            nc.vector.tensor_copy(out=picked2[:, tokens], in_=pe_rows[2][:].indirect(entries(tokens)))
+        for tokens in token_halves:
+            nc.vector.tensor_tensor(h_high[:, 0, tokens], first_banks[2][:, tokens], picked2[:, tokens], ADD)
 
         by_scalar = chunks[:-1] + [slice(chunks[-1].start, S - OWN)]
         for tokens in by_scalar:
@@ -155,6 +167,4 @@ def tile_picked_posadd_none_l_kernel(tc, xT, w1, w2_words, w2_scales, pe, offs, 
                 nc.vector.tensor_copy(out=result[:, tokens], in_=second_bank[:])
             else:
                 nc.scalar.copy(out=result[:, tokens], in_=second_bank[:])
-            if c > 0:
-                stored = slice(0, tokens.stop) if c == 1 else tokens
-                nc.sync.dma_start(out=out[:, stored], in_=result[:, stored])
+            nc.sync.dma_start(out=out[:, tokens], in_=result[:, tokens])

@@ -19,6 +19,7 @@ P = 128
 SLOTS = 4
 PAIRS = 2
 PER_COLUMN = 16
+BURST = 256
 QUADRANTS = 4
 CHUNK = 128
 CHUNKS = S // CHUNK
@@ -32,11 +33,11 @@ def tile_picked_posadd_none_l_kernel(tc, xT, w1, w2_words, w2_scales, pe, offs, 
         psum = ctx.enter_context(tc.psum_pool(name="psum", bufs=1))
 
         offsets = keep.tile([P, S // PER_COLUMN], U16, name="offsets")
-        w1_raw = keep.tile([P, SLOTS, H], F32, name="w1_raw")
-        x_pairs = [keep.tile([P, 2, T], F32, name="x_pairs%d" % u) for u in range(PAIRS)]
-        pe_low = keep.tile([P, 2, T], F32, name="pe_low")
-        pe_rows = {s: keep.tile([P, T], F32, name="pe_rows%d" % s) for s in (2, 3)}
-        w2_codes = keep.tile([P, 2 * N], U8, name="w2_codes", align_bytes=64)
+        w1_raw = keep.tile([P, SLOTS, H], F32, name="w1_raw", align_bytes=BURST)
+        x_pairs = [keep.tile([P, 2, T], F32, name="x_pairs%d" % u, align_bytes=BURST) for u in range(PAIRS)]
+        pe_low = keep.tile([P, 2, T], F32, name="pe_low", align_bytes=BURST)
+        pe_rows = {s: keep.tile([P, T], F32, name="pe_rows%d" % s, align_bytes=BURST) for s in (2, 3)}
+        w2_codes = keep.tile([P, 2 * N], U8, name="w2_codes", align_bytes=BURST)
         w2_scale_tile = keep.tile([P, N], U8, name="w2_scale_tile", align_bytes=64)
 
         def entries(tokens):
@@ -142,7 +143,7 @@ def tile_picked_posadd_none_l_kernel(tc, xT, w1, w2_words, w2_scales, pe, offs, 
             in_=h_high_row[:, S - OWN : S + OWN].rearrange("p (e c) -> p c e", e=2),
         )
 
-        result = keep.tile([P, S], F32, name="result")
+        result = keep.tile([P, S], F32, name="result", align_bytes=BURST)
         for c, tokens in enumerate(chunks):
             h_codes = keep.tile([P, CHUNK], U32, name="h_codes%d" % c, align_bytes=64)
             h_scale_tile = keep.tile([P, CHUNK], U8, name="h_scale_tile%d" % c, align_bytes=64)

@@ -19,7 +19,7 @@ P = 128
 SLOTS = 4
 PAIRS = 2
 PER_COLUMN = 16
-BURST = 256
+BURST = 4096
 QUADRANTS = 4
 CHUNK = 128
 CHUNKS = S // CHUNK
@@ -32,13 +32,13 @@ def tile_picked_posadd_none_l_kernel(tc, xT, w1, w2_words, w2_scales, pe, offs, 
         keep = ctx.enter_context(tc.tile_pool(name="keep", bufs=1))
         psum = ctx.enter_context(tc.psum_pool(name="psum", bufs=1))
 
-        offsets = keep.tile([P, S // PER_COLUMN], U16, name="offsets")
+        offsets = keep.tile([P, S // PER_COLUMN], U16, name="offsets", align_bytes=256)
         w1_raw = keep.tile([P, SLOTS, H], F32, name="w1_raw", align_bytes=BURST)
         x_pairs = [keep.tile([P, 2, T], F32, name="x_pairs%d" % u, align_bytes=BURST) for u in range(PAIRS)]
         pe_low = keep.tile([P, 2, T], F32, name="pe_low", align_bytes=BURST)
         pe_rows = {s: keep.tile([P, T], F32, name="pe_rows%d" % s, align_bytes=BURST) for s in (2, 3)}
-        w2_codes = keep.tile([P, 2 * N], U8, name="w2_codes", align_bytes=BURST)
-        w2_scale_tile = keep.tile([P, N], U8, name="w2_scale_tile", align_bytes=64)
+        w2_codes = keep.tile([P, 2 * N], U8, name="w2_codes", align_bytes=256)
+        w2_scale_tile = keep.tile([P, N], U8, name="w2_scale_tile", align_bytes=256)
 
         def entries(tokens):
             return offsets[:, tokens.start // PER_COLUMN : tokens.stop // PER_COLUMN]
@@ -143,7 +143,7 @@ def tile_picked_posadd_none_l_kernel(tc, xT, w1, w2_words, w2_scales, pe, offs, 
             in_=h_high_row[:, S - OWN : S + OWN].rearrange("p (e c) -> p c e", e=2),
         )
 
-        result = keep.tile([P, S], F32, name="result", align_bytes=BURST)
+        result = keep.tile([P, S], F32, name="result", align_bytes=256)
         for c, tokens in enumerate(chunks):
             h_codes = keep.tile([P, CHUNK], U32, name="h_codes%d" % c, align_bytes=64)
             h_scale_tile = keep.tile([P, CHUNK], U8, name="h_scale_tile%d" % c, align_bytes=64)

@@ -83,27 +83,28 @@ def tile_picked_posadd_none_l_kernel(tc, xT, w1, w2_words, w2_scales, pe, offs, 
                 in_=w1_raw[:].rearrange("p j (m s) -> p m j s", s=SLOTS)[:, :, :, 2 * u : 2 * u + 2],
             )
 
-        first_banks = []
+        def first_pass(s, bank_tag):
+            u, e = divmod(s, 2)
+            bank = psum.tile([P, S], F32, name="first_bank%d" % s, tag=bank_tag)
+            nc.tensor.matmul_mx(
+                out=bank[:],
+                lhsT=w1_codes[u][:, e * P : (e + 1) * P].bitcast(FP8X4),
+                lhsT_scale=w1_scale_tile[u][:, e * P : (e + 1) * P],
+                rhs=x_codes[:].bitcast(FP8X4),
+                rhs_scale=x_scale_tile[:],
+                start=True,
+                stop=True,
+            )
+            return bank
+
         for u in range(PAIRS):
             nc.vector.quantize_mx(out=w1_codes[u][:].bitcast(FP8X4), scales=w1_scale_tile[u][:], in_=w1_grouped[u][:])
-            for e in range(2):
-                first_bank = psum.tile([P, S], F32, name="first_bank%d" % (2 * u + e))
-                nc.tensor.matmul_mx(
-                    out=first_bank[:],
-                    lhsT=w1_codes[u][:, e * P : (e + 1) * P].bitcast(FP8X4),
-                    lhsT_scale=w1_scale_tile[u][:, e * P : (e + 1) * P],
-                    rhs=x_codes[:].bitcast(FP8X4),
-                    rhs_scale=x_scale_tile[:],
-                    start=True,
-                    stop=True,
-                )
-                first_banks.append(first_bank)
-
         projected_low = keep.tile([P, 2, S], F32, name="projected_low")
         for s in (0, 1):
-            nc.scalar.copy(out=projected_low[:, s, :], in_=first_banks[s][:])
+            nc.scalar.copy(out=projected_low[:, s, :], in_=first_pass(s, "low%d" % s)[:])
         projected = {3: keep.tile([P, S], F32, name="projected3")}
-        nc.scalar.copy(out=projected[3][:], in_=first_banks[3][:])
+        nc.scalar.copy(out=projected[3][:], in_=first_pass(3, "high")[:])
+        first_banks = {2: first_pass(2, "high")}
 
         h_high = keep.tile([P, 2, S], F32, name="h_high")
         h_grouped = [keep.tile([P, CHUNK, SLOTS], BF16, name="h_grouped%d" % c, align_bytes=64) for c in range(CHUNKS)]

@@ -114,7 +114,14 @@ def tile_picked_posadd_none_l_kernel(tc, xT, w1, w2_words, w2_scales, pe, offs, 
             picked_low = keep.tile([P, 2, S // 2], F32, name="picked_low%d" % half)
             for s in (0, 1):
                 nc.vector.tensor_copy(out=picked_low[:, s, :], in_=pe_low[:, s, :].indirect(entries(tokens)))
-                nc.gpsimd.tensor_tensor(h_low[:, s, tokens], picked_low[:, s, :], projected_low[:, s, tokens], ADD)
+                if half == 0:
+                    nc.gpsimd.tensor_tensor(h_low[:, s, tokens], picked_low[:, s, :], projected_low[:, s, tokens], ADD)
+            if half == 1:
+                for c in (2, 3):
+                    part = slice(chunks[c].start - tokens.start, chunks[c].stop - tokens.start)
+                    nc.gpsimd.tensor_tensor(
+                        h_low[:, :, chunks[c]], picked_low[:, :, part], projected_low[:, :, chunks[c]], ADD
+                    )
         for c, tokens in enumerate(chunks):
             nc.scalar.copy(out=h_grouped[c][:, :, 0:2], in_=h_low[:, :, tokens].rearrange("p e c -> p c e"))
 

@@ -33,11 +33,10 @@ def tile_picked_posadd_none_l_kernel(tc, xT, w1, w2_words, w2_scales, pe, offs, 
         psum = ctx.enter_context(tc.psum_pool(name="psum", bufs=1))
 
         offsets = keep.tile([P, S // PER_COLUMN], U16, name="offsets", align_bytes=256)
-        w1_raw = keep.tile([P, SLOTS, H], F32, name="w1_raw", align_bytes=BURST)
+        w1_raw = keep.tile([P, SLOTS, H], F32, name="w1_raw", tag="weights", align_bytes=BURST)
         x_pairs = [keep.tile([P, 2, T], F32, name="x_pairs%d" % u, align_bytes=BURST) for u in range(PAIRS)]
         pe_low = keep.tile([P, 2, T], F32, name="pe_low", align_bytes=BURST)
         pe_rows = {s: keep.tile([P, T], F32, name="pe_rows%d" % s, align_bytes=BURST) for s in (2, 3)}
-        w2_codes = keep.tile([P, 2 * N], U8, name="w2_codes", align_bytes=256)
         w2_scale_tile = keep.tile([P, N], U8, name="w2_scale_tile", align_bytes=256)
 
         def entries(tokens):
@@ -59,7 +58,6 @@ def tile_picked_posadd_none_l_kernel(tc, xT, w1, w2_words, w2_scales, pe, offs, 
         nc.sync.dma_start(out=pe_low[:], in_=pe.rearrange("(p u e) c -> u p e c", u=PAIRS, e=2)[0])
         for s in (2, 3):
             nc.sync.dma_start(out=pe_rows[s][:], in_=pe_by_slot[s])
-        nc.sync.dma_start(out=w2_codes[:].bitcast(I32), in_=w2_words[0].bitcast(I32))
 
         x_grouped = keep.tile([P, S, SLOTS], BF16, name="x_grouped", align_bytes=64)
         for s in range(SLOTS):
@@ -82,6 +80,9 @@ def tile_picked_posadd_none_l_kernel(tc, xT, w1, w2_words, w2_scales, pe, offs, 
                 out=w1_grouped[u][:].rearrange("p (e m j) -> p m j e", e=2, j=SLOTS),
                 in_=w1_raw[:].rearrange("p j (m s) -> p m j s", s=SLOTS)[:, :, :, 2 * u : 2 * u + 2],
             )
+
+        w2_codes = keep.tile([P, 2 * N], U8, name="w2_codes", tag="weights", align_bytes=BURST)
+        nc.sync.dma_start(out=w2_codes[:].bitcast(I32), in_=w2_words[0].bitcast(I32))
 
         def first_pass(s, bank_tag):
             u, e = divmod(s, 2)

@@ -173,7 +173,7 @@ def tile_picked_posadd_none_l_kernel(tc, xT, w1, w2_words, w2_scales, pe, offs, 
                 start=True,
                 stop=True,
             )
-            if c >= CHUNKS // 2:
+            if c == CHUNKS - 2:
                 nc.vector.tensor_copy(out=result[:, tokens], in_=second_bank[:])
             else:
                 nc.scalar.copy(out=result[:, tokens], in_=second_bank[:])

@@ -144,14 +144,6 @@ def tile_picked_posadd_none_l_kernel(tc, xT, w1, w2_words, w2_scales, pe, offs, 
                 in_=h_high[:, :, tokens].rearrange("p e c -> p c e"),
             )
 
-        own = slice(S - OWN, S)
-        nc.vector.tensor_tensor(h_high[:, 1, 0:OWN], pe_rows[3][:].indirect(entries(own)), projected[3][:, own], ADD)
-        h_high_row = h_high[:].rearrange("p e c -> p (e c)")
-        nc.vector.tensor_copy(
-            out=h_grouped[-1][:, CHUNK - OWN :, 2:4],
-            in_=h_high_row[:, S - OWN : S + OWN].rearrange("p (e c) -> p c e", e=2),
-        )
-
         result = keep.tile([P, S], F32, name="result", align_bytes=256)
         for c, tokens in enumerate(chunks):
             h_codes = keep.tile([P, CHUNK], U32, name="h_codes%d" % c, align_bytes=64)
@@ -162,6 +154,15 @@ def tile_picked_posadd_none_l_kernel(tc, xT, w1, w2_words, w2_scales, pe, offs, 
                     out=h_codes[:, part].bitcast(FP8X4),
                     scales=h_scale_tile[:, part],
                     in_=h_grouped[c][:, part, :].rearrange("p c s -> p (c s)"),
+                )
+            if c == 0:
+                own = slice(S - OWN, S)
+                nc.vector.tensor_tensor(h_high[:, 1, 0:OWN], pe_rows[3][:].indirect(entries(own)), projected[3][:, own], ADD)
+            if c == 1:
+                h_high_row = h_high[:].rearrange("p e c -> p (e c)")
+                nc.vector.tensor_copy(
+                    out=h_grouped[-1][:, CHUNK - OWN :, 2:4],
+                    in_=h_high_row[:, S - OWN : S + OWN].rearrange("p (e c) -> p c e", e=2),
                 )
             second_bank = psum.tile([P, CHUNK], F32, name="second_bank%d" % c)
             nc.tensor.matmul_mx(

@@ -14,6 +14,7 @@ U8 = mybir.dt.uint8
 FP8X4 = mybir.dt.float8_e4m3fn_x4
 FP4X4 = mybir.dt.float4_e2m1fn_x4
 ADD = mybir.AluOpType.add
+COPY = mybir.ActivationFunctionType.Copy
 
 P = 128
 SLOTS = 4
@@ -23,7 +24,7 @@ BURST = 4096
 QUADRANTS = 4
 CHUNK = 128
 CHUNKS = S // CHUNK
-OWN = CHUNK // 2
+HALF = S // 2
 
 
 def tile_picked_posadd_none_l_kernel(tc, xT, w1, w2_words, w2_scales, pe, offs, out):
@@ -68,13 +69,9 @@ def tile_picked_posadd_none_l_kernel(tc, xT, w1, w2_words, w2_scales, pe, offs, 
             out=x_codes[:].bitcast(FP8X4), scales=x_scale_tile[:], in_=x_grouped[:].rearrange("p c s -> p (c s)")
         )
 
-        w1_grouped = [
-            keep.tile([P, 2 * P * SLOTS], BF16, name="w1_grouped%d" % u, align_bytes=64)
-            for u in range(PAIRS)
-        ]
+        w1_grouped = [keep.tile([P, 2 * P * SLOTS], BF16, name="w1_grouped%d" % u, align_bytes=64) for u in range(PAIRS)]
         w1_codes = [keep.tile([P, 2 * P], U32, name="w1_codes%d" % u, align_bytes=64) for u in range(PAIRS)]
         w1_scale_tile = [keep.tile([P, 2 * P], U8, name="w1_scale_tile%d" % u, align_bytes=64) for u in range(PAIRS)]
-        h_low = keep.tile([P, 2, S], F32, name="h_low")
         for u in range(PAIRS):
             nc.scalar.copy(
                 out=w1_grouped[u][:].rearrange("p (e m j) -> p m j e", e=2, j=SLOTS),
@@ -84,98 +81,114 @@ def tile_picked_posadd_none_l_kernel(tc, xT, w1, w2_words, w2_scales, pe, offs, 
         w2_codes = keep.tile([P, 2 * N], U8, name="w2_codes", tag="weights", align_bytes=BURST)
         nc.sync.dma_start(out=w2_codes[:].bitcast(I32), in_=w2_words[0].bitcast(I32))
 
-        def first_pass(s, bank_tag):
+        def first_pass(s, tokens, bank):
             u, e = divmod(s, 2)
-            bank = psum.tile([P, S], F32, name="first_bank%d" % s, tag=bank_tag)
             nc.tensor.matmul_mx(
-                out=bank[:],
+                out=bank,
                 lhsT=w1_codes[u][:, e * P : (e + 1) * P].bitcast(FP8X4),
                 lhsT_scale=w1_scale_tile[u][:, e * P : (e + 1) * P],
-                rhs=x_codes[:].bitcast(FP8X4),
-                rhs_scale=x_scale_tile[:],
+                rhs=x_codes[:, tokens].bitcast(FP8X4),
+                rhs_scale=x_scale_tile[:, tokens],
                 start=True,
                 stop=True,
             )
-            return bank
 
         for u in range(PAIRS):
             nc.vector.quantize_mx(out=w1_codes[u][:].bitcast(FP8X4), scales=w1_scale_tile[u][:], in_=w1_grouped[u][:])
-        projected_low = keep.tile([P, 2, S], F32, name="projected_low")
-        for s in (0, 1):
-            nc.scalar.copy(out=projected_low[:, s, :], in_=first_pass(s, "low%d" % s)[:])
-        projected = {3: keep.tile([P, S], F32, name="projected3")}
-        nc.scalar.copy(out=projected[3][:], in_=first_pass(3, "high")[:])
-        first_banks = {2: first_pass(2, "high")}
+        halves = [slice(0, HALF), slice(HALF, S)]
+        chunks = [slice(c * CHUNK, (c + 1) * CHUNK) for c in range(CHUNKS)]
+        low_banks = [psum.tile([P, 2, HALF], F32, name="low_bank%d" % half) for half in range(2)]
+        for half, tokens in enumerate(halves):
+            for s in (0, 1):
+                first_pass(s, tokens, low_banks[half][:, s, :])
+        high_banks = {s: psum.tile([P, S], F32, name="high_bank%d" % s) for s in (2, 3)}
+        for s in (3, 2):
+            first_pass(s, slice(0, S), high_banks[s][:])
+        FUSED = 192
+        projected3 = keep.tile([P, FUSED], F32, name="projected3")
+        nc.scalar.copy(out=projected3[:], in_=high_banks[3][:, 0:FUSED])
+
+        h_grouped = [keep.tile([P, CHUNK, SLOTS], BF16, name="h_grouped%d" % c, align_bytes=64) for c in range(CHUNKS)]
+        picked_low = [keep.tile([P, 2, HALF], F32, name="picked_low%d" % half) for half in range(2)]
+        for half, tokens in enumerate(halves):
+            nc.vector.tensor_copy(out=picked_low[half][:, 0, :], in_=pe_low[:, 0, :].indirect(entries(tokens)))
+            nc.scalar.activation(picked_low[half][:, 1, :], pe_low[:, 1, :].indirect(entries(tokens)), COPY)
+        for c in range(CHUNKS):
+            half, part = c // 2, chunks[c % 2]
+            nc.vector.tensor_tensor(
+                h_grouped[c][:, :, 0:2],
+                low_banks[half][:, :, part].rearrange("p e c -> p c e"),
+                picked_low[half][:, :, part].rearrange("p e c -> p c e"),
+                ADD,
+            )
 
         h_high = keep.tile([P, 2, S], F32, name="h_high")
-        h_grouped = [keep.tile([P, CHUNK, SLOTS], BF16, name="h_grouped%d" % c, align_bytes=64) for c in range(CHUNKS)]
-        chunks = [slice(c * CHUNK, (c + 1) * CHUNK) for c in range(CHUNKS)]
-        for half in range(2):
-            tokens = slice(half * S // 2, (half + 1) * S // 2)
-            picked_low = keep.tile([P, 2, S // 2], F32, name="picked_low%d" % half)
-            for s in (0, 1):
-                nc.vector.tensor_copy(out=picked_low[:, s, :], in_=pe_low[:, s, :].indirect(entries(tokens)))
-                if half == 0:
-                    nc.gpsimd.tensor_tensor(h_low[:, s, tokens], picked_low[:, s, :], projected_low[:, s, tokens], ADD)
-            if half == 1:
-                for c in (2, 3):
-                    part = slice(chunks[c].start - tokens.start, chunks[c].stop - tokens.start)
-                    nc.gpsimd.tensor_tensor(
-                        h_low[:, :, chunks[c]], picked_low[:, :, part], projected_low[:, :, chunks[c]], ADD
-                    )
-        for c, tokens in enumerate(chunks):
-            nc.scalar.copy(out=h_grouped[c][:, :, 0:2], in_=h_low[:, :, tokens].rearrange("p e c -> p c e"))
-
         picked2 = keep.tile([P, S], F32, name="picked2")
-        token_halves = [slice(0, S // 2), slice(S // 2, S)]
-        for tokens in token_halves:
-            nc.vector.tensor_copy(out=picked2[:, tokens], in_=pe_rows[2][:].indirect(entries(tokens)))
-        for tokens in token_halves:
-            nc.vector.tensor_tensor(h_high[:, 0, tokens], first_banks[2][:, tokens], picked2[:, tokens], ADD)
+        for tokens in halves:
+            nc.scalar.activation(picked2[:, tokens], pe_rows[2][:].indirect(entries(tokens)), COPY)
+        for tokens in halves:
+            nc.vector.tensor_tensor(h_high[:, 0, tokens], high_banks[2][:, tokens], picked2[:, tokens], ADD)
 
-        by_scalar = chunks[:-1] + [slice(chunks[-1].start, S - OWN)]
-        for tokens in by_scalar:
-            nc.vector.tensor_tensor(
-                h_high[:, 1, tokens], pe_rows[3][:].indirect(entries(tokens)), projected[3][:, tokens], ADD
-            )
-        for c, tokens in enumerate(by_scalar):
-            nc.scalar.copy(
-                out=h_grouped[c][:, 0 : tokens.stop - tokens.start, 2:4],
-                in_=h_high[:, :, tokens].rearrange("p e c -> p c e"),
-            )
-
+        picked3 = keep.tile([P, S], F32, name="picked3")
         result = keep.tile([P, S], F32, name="result", align_bytes=256)
-        for c, tokens in enumerate(chunks):
-            h_codes = keep.tile([P, CHUNK], U32, name="h_codes%d" % c, align_bytes=64)
-            h_scale_tile = keep.tile([P, CHUNK], U8, name="h_scale_tile%d" % c, align_bytes=64)
-            last = c == CHUNKS - 1
-            for part in [slice(0, CHUNK - OWN), slice(CHUNK - OWN, CHUNK)] if last else [slice(0, CHUNK)]:
-                nc.vector.quantize_mx(
-                    out=h_codes[:, part].bitcast(FP8X4),
-                    scales=h_scale_tile[:, part],
-                    in_=h_grouped[c][:, part, :].rearrange("p c s -> p (c s)"),
-                )
-            if c == 0:
-                own = slice(S - OWN, S)
-                nc.vector.tensor_tensor(h_high[:, 1, 0:OWN], pe_rows[3][:].indirect(entries(own)), projected[3][:, own], ADD)
-            if c == 1:
-                h_high_row = h_high[:].rearrange("p e c -> p (e c)")
-                nc.vector.tensor_copy(
-                    out=h_grouped[-1][:, CHUNK - OWN :, 2:4],
-                    in_=h_high_row[:, S - OWN : S + OWN].rearrange("p (e c) -> p c e", e=2),
-                )
-            second_bank = psum.tile([P, CHUNK], F32, name="second_bank%d" % c)
+        h_codes = [keep.tile([P, CHUNK], U32, name="h_codes%d" % c, align_bytes=64) for c in range(CHUNKS)]
+        h_scale_tile = [keep.tile([P, CHUNK], U8, name="h_scale_tile%d" % c, align_bytes=64) for c in range(CHUNKS)]
+        second_banks = [psum.tile([P, CHUNK], F32, name="second_bank%d" % c) for c in range(CHUNKS)]
+
+        def fused(a, b):
+            nc.vector.tensor_tensor(h_high[:, 1, a:b], pe_rows[3][:].indirect(entries(slice(a, b))), projected3[:, a:b], ADD)
+
+        def pick(a, b):
+            nc.scalar.activation(picked3[:, a:b], pe_rows[3][:].indirect(entries(slice(a, b))), COPY)
+
+        def add(a, b):
+            nc.vector.tensor_tensor(h_high[:, 1, a:b], high_banks[3][:, a:b], picked3[:, a:b], ADD)
+
+        def lay(copy, a, b):
+            c = a // CHUNK
+            copy(out=h_grouped[c][:, a - c * CHUNK : b - c * CHUNK, 2:4], in_=h_high[:, :, a:b].rearrange("p e c -> p c e"))
+
+        def quantise(a, b):
+            c = a // CHUNK
+            part = slice(a - c * CHUNK, b - c * CHUNK)
+            nc.vector.quantize_mx(
+                out=h_codes[c][:, part].bitcast(FP8X4),
+                scales=h_scale_tile[c][:, part],
+                in_=h_grouped[c][:, part, :].rearrange("p c s -> p (c s)"),
+            )
+
+        def finish(c, copy):
             nc.tensor.matmul_mx(
-                out=second_bank[:],
+                out=second_banks[c][:],
                 lhsT=w2_codes[:].bitcast(FP4X4),
                 lhsT_scale=w2_scale_tile[:],
-                rhs=h_codes[:].bitcast(FP8X4),
-                rhs_scale=h_scale_tile[:],
+                rhs=h_codes[c][:].bitcast(FP8X4),
+                rhs_scale=h_scale_tile[c][:],
                 start=True,
                 stop=True,
             )
-            if c == CHUNKS - 2:
-                nc.vector.tensor_copy(out=result[:, tokens], in_=second_bank[:])
-            else:
-                nc.scalar.copy(out=result[:, tokens], in_=second_bank[:])
-            nc.sync.dma_start(out=out[:, tokens], in_=result[:, tokens])
+            copy(out=result[:, chunks[c]], in_=second_banks[c][:])
+            nc.sync.dma_start(out=out[:, chunks[c]], in_=result[:, chunks[c]])
+
+        SC, VC = nc.scalar.copy, nc.vector.tensor_copy
+        fused(0, 128)
+        pick(256, 384)
+        fused(128, 192)
+        pick(384, 512)
+        pick(192, 256)
+        add(256, 384)
+        add(384, 512)
+        add(192, 256)
+        lay(SC, 0, 128)
+        lay(SC, 128, 192)
+        lay(SC, 192, 256)
+        lay(VC, 256, 384)
+        lay(VC, 384, 512)
+        quantise(0, 128)
+        quantise(256, 384)
+        quantise(384, 512)
+        quantise(128, 256)
+        finish(0, SC)
+        finish(2, SC)
+        finish(3, VC)
+        finish(1, SC)

@@ -104,7 +104,7 @@ def tile_picked_posadd_none_l_kernel(tc, xT, w1, w2_words, w2_scales, pe, offs, 
         high_banks = {s: psum.tile([P, S], F32, name="high_bank%d" % s) for s in (2, 3)}
         for s in (3, 2):
             first_pass(s, slice(0, S), high_banks[s][:])
-        FUSED = 192
+        FUSED = 256
         projected3 = keep.tile([P, FUSED], F32, name="projected3")
         nc.scalar.copy(out=projected3[:], in_=high_banks[3][:, 0:FUSED])
 
@@ -124,8 +124,8 @@ def tile_picked_posadd_none_l_kernel(tc, xT, w1, w2_words, w2_scales, pe, offs, 
 
         h_high = keep.tile([P, 2, S], F32, name="h_high")
         picked2 = keep.tile([P, S], F32, name="picked2")
-        for tokens in halves:
-            nc.scalar.activation(picked2[:, tokens], pe_rows[2][:].indirect(entries(tokens)), COPY)
+        nc.scalar.activation(picked2[:, halves[0]], pe_rows[2][:].indirect(entries(halves[0])), COPY)
+        nc.vector.tensor_copy(out=picked2[:, halves[1]], in_=pe_rows[2][:].indirect(entries(halves[1])))
         for tokens in halves:
             nc.vector.tensor_tensor(h_high[:, 0, tokens], high_banks[2][:, tokens], picked2[:, tokens], ADD)
 
@@ -173,22 +173,22 @@ def tile_picked_posadd_none_l_kernel(tc, xT, w1, w2_words, w2_scales, pe, offs, 
         SC, VC = nc.scalar.copy, nc.vector.tensor_copy
         fused(0, 128)
         pick(256, 384)
-        fused(128, 192)
         pick(384, 512)
-        pick(192, 256)
+        fused(128, 192)
         add(256, 384)
+        fused(192, 256)
         add(384, 512)
-        add(192, 256)
         lay(SC, 0, 128)
         lay(SC, 128, 192)
         lay(SC, 192, 256)
+        lay(SC, 448, 512)
         lay(VC, 256, 384)
-        lay(VC, 384, 512)
         quantise(0, 128)
+        lay(VC, 384, 448)
         quantise(256, 384)
-        quantise(384, 512)
         quantise(128, 256)
+        quantise(384, 512)
         finish(0, SC)
-        finish(2, SC)
-        finish(3, VC)
-        finish(1, SC)
+        finish(2, VC)
+        finish(1, VC)
+        finish(3, SC)

@@ -124,8 +124,9 @@ def tile_picked_posadd_none_l_kernel(tc, xT, w1, w2_words, w2_scales, pe, offs, 
 
         h_high = keep.tile([P, 2, S], F32, name="h_high")
         picked2 = keep.tile([P, S], F32, name="picked2")
-        nc.scalar.activation(picked2[:, halves[0]], pe_rows[2][:].indirect(entries(halves[0])), COPY)
-        nc.vector.tensor_copy(out=picked2[:, halves[1]], in_=pe_rows[2][:].indirect(entries(halves[1])))
+        for tokens in (halves[0], chunks[2]):
+            nc.scalar.activation(picked2[:, tokens], pe_rows[2][:].indirect(entries(tokens)), COPY)
+        nc.vector.tensor_copy(out=picked2[:, chunks[3]], in_=pe_rows[2][:].indirect(entries(chunks[3])))
         for tokens in halves:
             nc.vector.tensor_tensor(h_high[:, 0, tokens], high_banks[2][:, tokens], picked2[:, tokens], ADD)
 

@@ -43,6 +43,8 @@ def tile_picked_posadd_none_l_kernel(tc, xT, w1, w2_words, w2_scales, pe, offs, 
         def entries(tokens):
             return offsets[:, tokens.start // PER_COLUMN : tokens.stop // PER_COLUMN]
 
+        nc.sync.dma_start(offsets[:], offs)
+        nc.scalar.dma_start(out=w1_raw[:], in_=w1.rearrange("(p j) c -> p j c", j=SLOTS))
         nc.vector.memset(w2_scale_tile[:].bitcast(I32), 0)
         for q in range(QUADRANTS):
             nc.scalar.dma_start(
@@ -52,10 +54,8 @@ def tile_picked_posadd_none_l_kernel(tc, xT, w1, w2_words, w2_scales, pe, offs, 
 
         x_by_pair = xT.rearrange("(p u e) c -> u p e c", u=PAIRS, e=2)
         pe_by_slot = pe.rearrange("(p s) c -> s p c", s=SLOTS)
-        nc.sync.dma_start(out=x_pairs[0][:], in_=x_by_pair[0])
-        nc.sync.dma_start(offsets[:], offs)
-        nc.sync.dma_start(out=x_pairs[1][:], in_=x_by_pair[1])
-        nc.sync.dma_start(out=w1_raw[:], in_=w1.rearrange("(p j) c -> p j c", j=SLOTS))
+        for u in range(PAIRS):
+            nc.sync.dma_start(out=x_pairs[u][:], in_=x_by_pair[u])
         nc.sync.dma_start(out=pe_low[:], in_=pe.rearrange("(p u e) c -> u p e c", u=PAIRS, e=2)[0])
         for s in (2, 3):
             nc.sync.dma_start(out=pe_rows[s][:], in_=pe_by_slot[s])
@@ -105,11 +105,9 @@ def tile_picked_posadd_none_l_kernel(tc, xT, w1, w2_words, w2_scales, pe, offs, 
         for s in (3, 2):
             first_pass(s, slice(0, S), high_banks[s][:])
         FUSED = 256
-        projected3 = keep.tile([P, FUSED], F32, name="projected3")
-        nc.scalar.copy(out=projected3[:], in_=high_banks[3][:, 0:FUSED])
 
         h_grouped = [keep.tile([P, CHUNK, SLOTS], BF16, name="h_grouped%d" % c, align_bytes=64) for c in range(CHUNKS)]
-        picked_low = [keep.tile([P, 2, HALF], F32, name="picked_low%d" % half) for half in range(2)]
+        picked_low = [keep.tile([P, 2, HALF], F32, name="picked_low%d" % half, tag="picked%d" % half) for half in range(2)]
         for half, tokens in enumerate(halves):
             nc.vector.tensor_copy(out=picked_low[half][:, 0, :], in_=pe_low[:, 0, :].indirect(entries(tokens)))
             nc.scalar.activation(picked_low[half][:, 1, :], pe_low[:, 1, :].indirect(entries(tokens)), COPY)
@@ -121,6 +119,9 @@ def tile_picked_posadd_none_l_kernel(tc, xT, w1, w2_words, w2_scales, pe, offs, 
                 picked_low[half][:, :, part].rearrange("p e c -> p c e"),
                 ADD,
             )
+
+        projected3 = keep.tile([P, FUSED], F32, name="projected3", tag="picked0")
+        nc.scalar.copy(out=projected3[:], in_=high_banks[3][:, 0:FUSED])
 
         h_high = keep.tile([P, 2, S], F32, name="h_high")
         picked2 = keep.tile([P, S], F32, name="picked2")

@@ -34,17 +34,15 @@ def tile_picked_posadd_none_l_kernel(tc, xT, w1, w2_words, w2_scales, pe, offs, 
         psum = ctx.enter_context(tc.psum_pool(name="psum", bufs=1))
 
         offsets = keep.tile([P, S // PER_COLUMN], U16, name="offsets", align_bytes=256)
-        w1_raw = keep.tile([P, SLOTS, H], F32, name="w1_raw", tag="weights", align_bytes=BURST)
-        x_pairs = [keep.tile([P, 2, T], F32, name="x_pairs%d" % u, align_bytes=BURST) for u in range(PAIRS)]
-        pe_low = keep.tile([P, 2, T], F32, name="pe_low", align_bytes=BURST)
+        w1_raw = keep.tile([P, SLOTS, H], F32, name="w1_raw", align_bytes=BURST)
+        x_rows = keep.tile([P, SLOTS, T], F32, name="x_rows", align_bytes=BURST)
+        pe_low = keep.tile([P, 2, T], F32, name="pe_low", tag="low", align_bytes=BURST)
         pe_rows = {s: keep.tile([P, T], F32, name="pe_rows%d" % s, align_bytes=BURST) for s in (2, 3)}
         w2_scale_tile = keep.tile([P, N], U8, name="w2_scale_tile", align_bytes=256)
 
         def entries(tokens):
             return offsets[:, tokens.start // PER_COLUMN : tokens.stop // PER_COLUMN]
 
-        nc.sync.dma_start(offsets[:], offs)
-        nc.scalar.dma_start(out=w1_raw[:], in_=w1.rearrange("(p j) c -> p j c", j=SLOTS))
         nc.vector.memset(w2_scale_tile[:].bitcast(I32), 0)
         for q in range(QUADRANTS):
             nc.scalar.dma_start(
@@ -52,22 +50,32 @@ def tile_picked_posadd_none_l_kernel(tc, xT, w1, w2_words, w2_scales, pe, offs, 
                 in_=w2_scales[0, 4 * q : 4 * q + 4, :].bitcast(I32),
             )
 
-        x_by_pair = xT.rearrange("(p u e) c -> u p e c", u=PAIRS, e=2)
         pe_by_slot = pe.rearrange("(p s) c -> s p c", s=SLOTS)
-        for u in range(PAIRS):
-            nc.sync.dma_start(out=x_pairs[u][:], in_=x_by_pair[u])
+        nc.sync.dma_start(out=w1_raw[:], in_=w1.rearrange("(p j) c -> p j c", j=SLOTS))
+        nc.sync.dma_start(offsets[:], offs)
+        nc.sync.dma_start(out=x_rows[:], in_=xT.rearrange("(p s) c -> p s c", s=SLOTS))
         nc.sync.dma_start(out=pe_low[:], in_=pe.rearrange("(p u e) c -> u p e c", u=PAIRS, e=2)[0])
         for s in (2, 3):
             nc.sync.dma_start(out=pe_rows[s][:], in_=pe_by_slot[s])
 
-        x_grouped = keep.tile([P, S, SLOTS], BF16, name="x_grouped", align_bytes=64)
-        for s in range(SLOTS):
-            nc.vector.tensor_copy(out=x_grouped[:, :, s], in_=x_pairs[s // 2][:, s % 2, :].indirect(offsets[:]))
+        halves = [slice(0, HALF), slice(HALF, S)]
+        x_picked = [keep.tile([P, SLOTS, HALF], F32, name="x_picked%d" % half) for half in range(2)]
+        x_grouped = [keep.tile([P, HALF, SLOTS], BF16, name="x_grouped%d" % half, align_bytes=64) for half in range(2)]
         x_codes = keep.tile([P, S], U32, name="x_codes", align_bytes=64)
         x_scale_tile = keep.tile([P, S], U8, name="x_scale_tile", align_bytes=64)
-        nc.vector.quantize_mx(
-            out=x_codes[:].bitcast(FP8X4), scales=x_scale_tile[:], in_=x_grouped[:].rearrange("p c s -> p (c s)")
-        )
+        for half, tokens in enumerate(halves):
+            for s in (0, 1):
+                nc.vector.tensor_copy(out=x_picked[half][:, s, :], in_=x_rows[:, s, :].indirect(entries(tokens)))
+            for s in (2, 3):
+                nc.scalar.activation(x_picked[half][:, s, :], x_rows[:, s, :].indirect(entries(tokens)), COPY)
+        for half in range(2):
+            nc.vector.tensor_copy(out=x_grouped[half][:], in_=x_picked[half][:].rearrange("p s c -> p c s"))
+        for half, tokens in enumerate(halves):
+            nc.vector.quantize_mx(
+                out=x_codes[:, tokens].bitcast(FP8X4),
+                scales=x_scale_tile[:, tokens],
+                in_=x_grouped[half][:].rearrange("p c s -> p (c s)"),
+            )
 
         w1_grouped = [keep.tile([P, 2 * P * SLOTS], BF16, name="w1_grouped%d" % u, align_bytes=64) for u in range(PAIRS)]
         w1_codes = [keep.tile([P, 2 * P], U32, name="w1_codes%d" % u, align_bytes=64) for u in range(PAIRS)]
@@ -77,9 +85,6 @@ def tile_picked_posadd_none_l_kernel(tc, xT, w1, w2_words, w2_scales, pe, offs, 
                 out=w1_grouped[u][:].rearrange("p (e m j) -> p m j e", e=2, j=SLOTS),
                 in_=w1_raw[:].rearrange("p j (m s) -> p m j s", s=SLOTS)[:, :, :, 2 * u : 2 * u + 2],
             )
-
-        w2_codes = keep.tile([P, 2 * N], U8, name="w2_codes", tag="weights", align_bytes=BURST)
-        nc.sync.dma_start(out=w2_codes[:].bitcast(I32), in_=w2_words[0].bitcast(I32))
 
         def first_pass(s, tokens, bank):
             u, e = divmod(s, 2)
@@ -95,7 +100,6 @@ def tile_picked_posadd_none_l_kernel(tc, xT, w1, w2_words, w2_scales, pe, offs, 
 
         for u in range(PAIRS):
             nc.vector.quantize_mx(out=w1_codes[u][:].bitcast(FP8X4), scales=w1_scale_tile[u][:], in_=w1_grouped[u][:])
-        halves = [slice(0, HALF), slice(HALF, S)]
         chunks = [slice(c * CHUNK, (c + 1) * CHUNK) for c in range(CHUNKS)]
         low_banks = [psum.tile([P, 2, HALF], F32, name="low_bank%d" % half) for half in range(2)]
         for half, tokens in enumerate(halves):
@@ -119,6 +123,10 @@ def tile_picked_posadd_none_l_kernel(tc, xT, w1, w2_words, w2_scales, pe, offs, 
                 picked_low[half][:, :, part].rearrange("p e c -> p c e"),
                 ADD,
             )
+
+        w2_codes = keep.tile([P, 2 * N], U8, name="w2_codes", tag="low", align_bytes=BURST)
+        for rows in (slice(0, P // 2), slice(P // 2, P)):
+            nc.sync.dma_start(out=w2_codes[rows, :].bitcast(I32), in_=w2_words[0, rows, :].bitcast(I32))
 
         projected3 = keep.tile([P, FUSED], F32, name="projected3", tag="picked0")
         nc.scalar.copy(out=projected3[:], in_=high_banks[3][:, 0:FUSED])

@@ -31,12 +31,13 @@ def tile_picked_posadd_none_l_kernel(tc, xT, w1, w2_words, w2_scales, pe, offs, 
     nc = tc.nc
     with ExitStack() as ctx:
         keep = ctx.enter_context(tc.tile_pool(name="keep", bufs=1))
+        reused = ctx.enter_context(tc.tile_pool(name="reused", bufs=1))
         psum = ctx.enter_context(tc.psum_pool(name="psum", bufs=1))
 
         offsets = keep.tile([P, S // PER_COLUMN], U16, name="offsets", align_bytes=256)
         w1_raw = keep.tile([P, SLOTS, H], F32, name="w1_raw", align_bytes=BURST)
         x_rows = keep.tile([P, SLOTS, T], F32, name="x_rows", align_bytes=BURST)
-        pe_low = keep.tile([P, 2, T], F32, name="pe_low", tag="low", align_bytes=BURST)
+        pe_low = reused.tile([P, 2, T], F32, name="pe_low", offset=0, align_bytes=BURST)
         pe_rows = {s: keep.tile([P, T], F32, name="pe_rows%d" % s, align_bytes=BURST) for s in (2, 3)}
         w2_scale_tile = keep.tile([P, N], U8, name="w2_scale_tile", align_bytes=256)
 
@@ -111,7 +112,7 @@ def tile_picked_posadd_none_l_kernel(tc, xT, w1, w2_words, w2_scales, pe, offs, 
         FUSED = 256
 
         h_grouped = [keep.tile([P, CHUNK, SLOTS], BF16, name="h_grouped%d" % c, align_bytes=64) for c in range(CHUNKS)]
-        picked_low = [keep.tile([P, 2, HALF], F32, name="picked_low%d" % half, tag="picked%d" % half) for half in range(2)]
+        picked_low = [keep.tile([P, 2, HALF], F32, name="picked_low%d" % half) for half in range(2)]
         for half, tokens in enumerate(halves):
             nc.vector.tensor_copy(out=picked_low[half][:, 0, :], in_=pe_low[:, 0, :].indirect(entries(tokens)))
             nc.scalar.activation(picked_low[half][:, 1, :], pe_low[:, 1, :].indirect(entries(tokens)), COPY)
@@ -124,11 +125,11 @@ def tile_picked_posadd_none_l_kernel(tc, xT, w1, w2_words, w2_scales, pe, offs, 
                 ADD,
             )
 
-        w2_codes = keep.tile([P, 2 * N], U8, name="w2_codes", tag="low", align_bytes=BURST)
+        w2_codes = reused.tile([P, 2 * N], U8, name="w2_codes", offset=0, align_bytes=BURST)
         for rows in (slice(0, P // 2), slice(P // 2, P)):
             nc.sync.dma_start(out=w2_codes[rows, :].bitcast(I32), in_=w2_words[0, rows, :].bitcast(I32))
 
-        projected3 = keep.tile([P, FUSED], F32, name="projected3", tag="picked0")
+        projected3 = reused.tile([P, FUSED], F32, name="projected3", offset=BURST, align_bytes=BURST)
         nc.scalar.copy(out=projected3[:], in_=high_banks[3][:, 0:FUSED])
 
         h_high = keep.tile([P, 2, S], F32, name="h_high")

@@ -70,7 +70,10 @@ def tile_picked_posadd_none_l_kernel(tc, xT, w1, w2_words, w2_scales, pe, offs, 
             for s in (2, 3):
                 nc.scalar.activation(x_picked[half][:, s, :], x_rows[:, s, :].indirect(entries(tokens)), COPY)
         for half in range(2):
-            nc.vector.tensor_copy(out=x_grouped[half][:], in_=x_picked[half][:].rearrange("p s c -> p c s"))
+            nc.vector.tensor_copy(
+                out=x_grouped[half][:].rearrange("p (c i) s -> p c s i", i=4),
+                in_=x_picked[half][:].rearrange("p s (c i) -> p c s i", i=4),
+            )
         for half, tokens in enumerate(halves):
             nc.vector.quantize_mx(
                 out=x_codes[:, tokens].bitcast(FP8X4),
@@ -103,13 +106,11 @@ def tile_picked_posadd_none_l_kernel(tc, xT, w1, w2_words, w2_scales, pe, offs, 
             nc.vector.quantize_mx(out=w1_codes[u][:].bitcast(FP8X4), scales=w1_scale_tile[u][:], in_=w1_grouped[u][:])
         chunks = [slice(c * CHUNK, (c + 1) * CHUNK) for c in range(CHUNKS)]
         low_banks = [psum.tile([P, 2, HALF], F32, name="low_bank%d" % half) for half in range(2)]
+        high_banks = [psum.tile([P, 2, HALF], F32, name="high_bank%d" % half) for half in range(2)]
         for half, tokens in enumerate(halves):
-            for s in (0, 1):
-                first_pass(s, tokens, low_banks[half][:, s, :])
-        high_banks = {s: psum.tile([P, S], F32, name="high_bank%d" % s) for s in (2, 3)}
-        for s in (3, 2):
-            first_pass(s, slice(0, S), high_banks[s][:])
-        FUSED = 256
+            for s in range(SLOTS):
+                first_pass(s, tokens, (low_banks, high_banks)[s // 2][half][:, s % 2, :])
+        FUSED = HALF
 
         h_grouped = [keep.tile([P, CHUNK, SLOTS], BF16, name="h_grouped%d" % c, align_bytes=64) for c in range(CHUNKS)]
         picked_low = [keep.tile([P, 2, HALF], F32, name="picked_low%d" % half) for half in range(2)]
@@ -130,15 +131,15 @@ def tile_picked_posadd_none_l_kernel(tc, xT, w1, w2_words, w2_scales, pe, offs, 
             nc.sync.dma_start(out=w2_codes[rows, :].bitcast(I32), in_=w2_words[0, rows, :].bitcast(I32))
 
         projected3 = reused.tile([P, FUSED], F32, name="projected3", offset=BURST, align_bytes=BURST)
-        nc.scalar.copy(out=projected3[:], in_=high_banks[3][:, 0:FUSED])
+        nc.scalar.copy(out=projected3[:], in_=high_banks[0][:, 1, :])
 
         h_high = keep.tile([P, 2, S], F32, name="h_high")
         picked2 = keep.tile([P, S], F32, name="picked2")
         for tokens in (halves[0], chunks[2]):
             nc.scalar.activation(picked2[:, tokens], pe_rows[2][:].indirect(entries(tokens)), COPY)
         nc.vector.tensor_copy(out=picked2[:, chunks[3]], in_=pe_rows[2][:].indirect(entries(chunks[3])))
-        for tokens in halves:
-            nc.vector.tensor_tensor(h_high[:, 0, tokens], high_banks[2][:, tokens], picked2[:, tokens], ADD)
+        for half, tokens in enumerate(halves):
+            nc.vector.tensor_tensor(h_high[:, 0, tokens], high_banks[half][:, 0, :], picked2[:, tokens], ADD)
 
         picked3 = keep.tile([P, S], F32, name="picked3")
         result = keep.tile([P, S], F32, name="result", align_bytes=256)
@@ -153,7 +154,7 @@ def tile_picked_posadd_none_l_kernel(tc, xT, w1, w2_words, w2_scales, pe, offs, 
             nc.scalar.activation(picked3[:, a:b], pe_rows[3][:].indirect(entries(slice(a, b))), COPY)
 
         def add(a, b):
-            nc.vector.tensor_tensor(h_high[:, 1, a:b], high_banks[3][:, a:b], picked3[:, a:b], ADD)
+            nc.vector.tensor_tensor(h_high[:, 1, a:b], high_banks[1][:, 1, a - HALF : b - HALF], picked3[:, a:b], ADD)
 
         def lay(copy, a, b):
             c = a // CHUNK

from contextlib import ExitStack

import concourse.mybir as mybir

K, T, S, H, N = 512, 2048, 512, 512, 128
FLOPS = 2 * K * H * S + 2 * H * N * S

F32 = mybir.dt.float32
BF16 = mybir.dt.bfloat16
I32 = mybir.dt.int32
U32 = mybir.dt.uint32
U16 = mybir.dt.uint16
U8 = mybir.dt.uint8
FP8X4 = mybir.dt.float8_e4m3fn_x4
FP4X4 = mybir.dt.float4_e2m1fn_x4
ADD = mybir.AluOpType.add
COPY = mybir.ActivationFunctionType.Copy

P = 128
SLOTS = 4
PAIRS = 2
PER_COLUMN = 16
BURST = 4096
QUADRANTS = 4
CHUNK = 128
CHUNKS = S // CHUNK
HALF = S // 2


def tile_picked_posadd_none_l_kernel(tc, xT, w1, w2_words, w2_scales, pe, offs, out):
    nc = tc.nc
    with ExitStack() as ctx:
        keep = ctx.enter_context(tc.tile_pool(name="keep", bufs=1))
        reused = ctx.enter_context(tc.tile_pool(name="reused", bufs=1))
        psum = ctx.enter_context(tc.psum_pool(name="psum", bufs=1))

        offsets = keep.tile([P, S // PER_COLUMN], U16, name="offsets", align_bytes=256)
        w1_raw = keep.tile([P, SLOTS, H], F32, name="w1_raw", align_bytes=BURST)
        x_rows = keep.tile([P, SLOTS, T], F32, name="x_rows", align_bytes=BURST)
        pe_low = reused.tile([P, 2, T], F32, name="pe_low", offset=0, align_bytes=BURST)
        pe_rows = {s: keep.tile([P, T], F32, name="pe_rows%d" % s, align_bytes=BURST) for s in (2, 3)}
        w2_scale_tile = keep.tile([P, N], U8, name="w2_scale_tile", align_bytes=256)

        def entries(tokens):
            return offsets[:, tokens.start // PER_COLUMN : tokens.stop // PER_COLUMN]

        nc.vector.memset(w2_scale_tile[:].bitcast(I32), 0)
        for q in range(QUADRANTS):
            nc.scalar.dma_start(
                out=w2_scale_tile[32 * q : 32 * q + 4, :].bitcast(I32),
                in_=w2_scales[0, 4 * q : 4 * q + 4, :].bitcast(I32),
            )

        pe_by_slot = pe.rearrange("(p s) c -> s p c", s=SLOTS)
        nc.sync.dma_start(out=w1_raw[:], in_=w1.rearrange("(p j) c -> p j c", j=SLOTS))
        nc.sync.dma_start(offsets[:], offs)
        nc.sync.dma_start(out=x_rows[:], in_=xT.rearrange("(p s) c -> p s c", s=SLOTS))
        nc.sync.dma_start(out=pe_low[:], in_=pe.rearrange("(p u e) c -> u p e c", u=PAIRS, e=2)[0])
        for s in (2, 3):
            nc.sync.dma_start(out=pe_rows[s][:], in_=pe_by_slot[s])

        halves = [slice(0, HALF), slice(HALF, S)]
        x_picked = [keep.tile([P, SLOTS, HALF], F32, name="x_picked%d" % half) for half in range(2)]
        x_grouped = [keep.tile([P, HALF, SLOTS], BF16, name="x_grouped%d" % half, align_bytes=64) for half in range(2)]
        x_codes = keep.tile([P, S], U32, name="x_codes", align_bytes=64)
        x_scale_tile = keep.tile([P, S], U8, name="x_scale_tile", align_bytes=64)
        for half, tokens in enumerate(halves):
            for s in (0, 1):
                nc.vector.tensor_copy(out=x_picked[half][:, s, :], in_=x_rows[:, s, :].indirect(entries(tokens)))
            for s in (2, 3):
                nc.scalar.activation(x_picked[half][:, s, :], x_rows[:, s, :].indirect(entries(tokens)), COPY)
        for half in range(2):
            nc.vector.tensor_copy(
                out=x_grouped[half][:].rearrange("p (c i) s -> p c s i", i=4),
                in_=x_picked[half][:].rearrange("p s (c i) -> p c s i", i=4),
            )
        for half, tokens in enumerate(halves):
            nc.vector.quantize_mx(
                out=x_codes[:, tokens].bitcast(FP8X4),
                scales=x_scale_tile[:, tokens],
                in_=x_grouped[half][:].rearrange("p c s -> p (c s)"),
            )

        w1_grouped = [keep.tile([P, 2 * P * SLOTS], BF16, name="w1_grouped%d" % u, align_bytes=64) for u in range(PAIRS)]
        w1_codes = [keep.tile([P, 2 * P], U32, name="w1_codes%d" % u, align_bytes=64) for u in range(PAIRS)]
        w1_scale_tile = [keep.tile([P, 2 * P], U8, name="w1_scale_tile%d" % u, align_bytes=64) for u in range(PAIRS)]
        for u in range(PAIRS):
            nc.scalar.copy(
                out=w1_grouped[u][:].rearrange("p (e m j) -> p m j e", e=2, j=SLOTS),
                in_=w1_raw[:].rearrange("p j (m s) -> p m j s", s=SLOTS)[:, :, :, 2 * u : 2 * u + 2],
            )

        def first_pass(s, tokens, bank):
            u, e = divmod(s, 2)
            nc.tensor.matmul_mx(
                out=bank,
                lhsT=w1_codes[u][:, e * P : (e + 1) * P].bitcast(FP8X4),
                lhsT_scale=w1_scale_tile[u][:, e * P : (e + 1) * P],
                rhs=x_codes[:, tokens].bitcast(FP8X4),
                rhs_scale=x_scale_tile[:, tokens],
                start=True,
                stop=True,
            )

        for u in range(PAIRS):
            nc.vector.quantize_mx(out=w1_codes[u][:].bitcast(FP8X4), scales=w1_scale_tile[u][:], in_=w1_grouped[u][:])
        chunks = [slice(c * CHUNK, (c + 1) * CHUNK) for c in range(CHUNKS)]
        low_banks = [psum.tile([P, 2, HALF], F32, name="low_bank%d" % half) for half in range(2)]
        high_banks = [psum.tile([P, 2, HALF], F32, name="high_bank%d" % half) for half in range(2)]
        for half, tokens in enumerate(halves):
            for s in range(SLOTS):
                first_pass(s, tokens, (low_banks, high_banks)[s // 2][half][:, s % 2, :])
        FUSED = HALF

        h_grouped = [keep.tile([P, CHUNK, SLOTS], BF16, name="h_grouped%d" % c, align_bytes=64) for c in range(CHUNKS)]
        picked_low = [keep.tile([P, 2, HALF], F32, name="picked_low%d" % half) for half in range(2)]
        for half, tokens in enumerate(halves):
            nc.vector.tensor_copy(out=picked_low[half][:, 0, :], in_=pe_low[:, 0, :].indirect(entries(tokens)))
            nc.scalar.activation(picked_low[half][:, 1, :], pe_low[:, 1, :].indirect(entries(tokens)), COPY)
        for c in range(CHUNKS):
            half, part = c // 2, chunks[c % 2]
            nc.vector.tensor_tensor(
                h_grouped[c][:, :, 0:2],
                low_banks[half][:, :, part].rearrange("p e c -> p c e"),
                picked_low[half][:, :, part].rearrange("p e c -> p c e"),
                ADD,
            )

        w2_codes = reused.tile([P, 2 * N], U8, name="w2_codes", offset=0, align_bytes=BURST)
        for rows in (slice(0, P // 2), slice(P // 2, P)):
            nc.sync.dma_start(out=w2_codes[rows, :].bitcast(I32), in_=w2_words[0, rows, :].bitcast(I32))

        projected3 = reused.tile([P, FUSED], F32, name="projected3", offset=BURST, align_bytes=BURST)
        nc.scalar.copy(out=projected3[:], in_=high_banks[0][:, 1, :])

        h_high = keep.tile([P, 2, S], F32, name="h_high")
        picked2 = keep.tile([P, S], F32, name="picked2")
        for tokens in (halves[0], chunks[2]):
            nc.scalar.activation(picked2[:, tokens], pe_rows[2][:].indirect(entries(tokens)), COPY)
        nc.vector.tensor_copy(out=picked2[:, chunks[3]], in_=pe_rows[2][:].indirect(entries(chunks[3])))
        for half, tokens in enumerate(halves):
            nc.vector.tensor_tensor(h_high[:, 0, tokens], high_banks[half][:, 0, :], picked2[:, tokens], ADD)

        picked3 = keep.tile([P, S], F32, name="picked3")
        result = keep.tile([P, S], F32, name="result", align_bytes=256)
        h_codes = [keep.tile([P, CHUNK], U32, name="h_codes%d" % c, align_bytes=64) for c in range(CHUNKS)]
        h_scale_tile = [keep.tile([P, CHUNK], U8, name="h_scale_tile%d" % c, align_bytes=64) for c in range(CHUNKS)]
        second_banks = [psum.tile([P, CHUNK], F32, name="second_bank%d" % c) for c in range(CHUNKS)]

        def fused(a, b):
            nc.vector.tensor_tensor(h_high[:, 1, a:b], pe_rows[3][:].indirect(entries(slice(a, b))), projected3[:, a:b], ADD)

        def pick(a, b):
            nc.scalar.activation(picked3[:, a:b], pe_rows[3][:].indirect(entries(slice(a, b))), COPY)

        def add(a, b):
            nc.vector.tensor_tensor(h_high[:, 1, a:b], high_banks[1][:, 1, a - HALF : b - HALF], picked3[:, a:b], ADD)

        def lay(copy, a, b):
            c = a // CHUNK
            copy(out=h_grouped[c][:, a - c * CHUNK : b - c * CHUNK, 2:4], in_=h_high[:, :, a:b].rearrange("p e c -> p c e"))

        def quantise(a, b):
            c = a // CHUNK
            part = slice(a - c * CHUNK, b - c * CHUNK)
            nc.vector.quantize_mx(
                out=h_codes[c][:, part].bitcast(FP8X4),
                scales=h_scale_tile[c][:, part],
                in_=h_grouped[c][:, part, :].rearrange("p c s -> p (c s)"),
            )

        def finish(c, copy):
            nc.tensor.matmul_mx(
                out=second_banks[c][:],
                lhsT=w2_codes[:].bitcast(FP4X4),
                lhsT_scale=w2_scale_tile[:],
                rhs=h_codes[c][:].bitcast(FP8X4),
                rhs_scale=h_scale_tile[c][:],
                start=True,
                stop=True,
            )
            copy(out=result[:, chunks[c]], in_=second_banks[c][:])
            nc.sync.dma_start(out=out[:, chunks[c]], in_=result[:, chunks[c]])

        SC, VC = nc.scalar.copy, nc.vector.tensor_copy
        fused(0, 128)
        pick(256, 384)
        pick(384, 512)
        fused(128, 192)
        add(256, 384)
        fused(192, 256)
        add(384, 512)
        lay(SC, 0, 128)
        lay(SC, 128, 192)
        lay(SC, 192, 256)
        lay(SC, 448, 512)
        lay(VC, 256, 384)
        quantise(0, 128)
        lay(VC, 384, 448)
        quantise(256, 384)
        quantise(128, 256)
        quantise(384, 512)
        finish(0, SC)
        finish(2, VC)
        finish(1, VC)
        finish(3, SC)
